import numpy as np
import ml_dtypes


def mxq(x, axis, fmt="e4m3"):
    dtype, down = {"e4m3": (ml_dtypes.float8_e4m3fn, 7), "e5m2": (ml_dtypes.float8_e5m2, 14)}[fmt]
    v = np.moveaxis(np.asarray(x, np.float32).astype(ml_dtypes.bfloat16).astype(np.float64), axis, -1)
    blocks = v.reshape(v.shape[:-1] + (-1, 32))
    amax = np.abs(blocks).max(-1, keepdims=True)
    byte = np.maximum(np.where(amax > 0, np.frexp(amax)[1] - 1 + 127, 0) - down, 1)
    scale = np.exp2(byte - 127.0)
    codes = (blocks / scale).astype(np.float32).astype(dtype).astype(np.float64)
    return np.moveaxis((codes * scale).reshape(v.shape), -1, axis)


WIDE = False


def mx_kscale(k):
    if not WIDE:
        return np.ones(k)
    levels = np.array([10, -10, 5, -5, 0])
    if k % 512:
        return np.exp2(np.random.permutation(np.resize(levels, k // 32))).repeat(32)
    a = np.empty((k // 512, 16))
    for p in range(k // 512):
        a[p, :8] = np.random.permutation(np.resize(levels, 8))
        for g in range(8):
            far = levels[np.abs(levels - a[p, g]) >= 10]
            a[p, g + 8] = far[np.random.randint(len(far))]
    return np.exp2(a.ravel()).repeat(32)


def f64(x):
    return np.asarray(x).astype(np.float64)


def striped(idx):
    return np.tile(idx.reshape(-1, 16).T, (8, 1)).astype(np.uint16)


def unstriped(offs):
    return offs[:16].T.reshape(-1).astype(np.int64)


E2M1 = np.array([0.0, 0.5, 1.0, 1.5, 2.0, 3.0, 4.0, 6.0, -0.0, -0.5, -1.0, -1.5, -2.0, -3.0, -4.0, -6.0])


def pack_weight(w, fmt):
    k, n = w.shape
    w = f64(np.asarray(w, np.float32).astype(ml_dtypes.bfloat16)).reshape(k // 32, 32, n)
    amax = np.abs(w).max(1)
    if fmt == "e4m3":
        byte = np.frexp(amax)[1] - 1 + 127 - 7
    else:
        mant, ex = np.frexp(amax / 6.0)
        byte = np.where(mant > 0.5, ex, ex - 1) + 127
    byte = np.clip(np.where(amax > 0, byte, 1), 1, 254)
    scaled = (w * np.exp2(127.0 - byte)[:, None, :]).reshape(k, n).astype(np.float32)
    by_word = np.ascontiguousarray(scaled.reshape(k // 512, 128, 4, n).transpose(0, 1, 3, 2))
    if fmt == "e4m3":
        words = by_word.astype(ml_dtypes.float8_e4m3fn).view(np.uint8)
    else:
        c = by_word.astype(ml_dtypes.float4_e2m1fn).view(np.uint8) & 0xF
        words = (c[..., 0::2] | (c[..., 1::2] << 4)).reshape(k // 512, 128, 2 * n)
    return np.ascontiguousarray(words), np.ascontiguousarray(byte.astype(np.uint8).reshape(k // 512, 16, n))


def unpack_weight(words, scales, fmt):
    g, _, n = scales.shape
    words = np.ascontiguousarray(words).reshape(g, 128, n, -1)
    if fmt == "e4m3":
        vals = words.view(ml_dtypes.float8_e4m3fn).astype(np.float64)
    else:
        nib = np.empty((g, 128, n, 4), np.uint8)
        nib[..., 0::2] = words & 0xF
        nib[..., 1::2] = words >> 4
        vals = E2M1[nib]
    vals = vals * np.repeat(np.exp2(scales.astype(np.float64) - 127.0), 8, axis=1)[..., None]
    return vals.transpose(0, 1, 3, 2).reshape(g * 512, n)


def gelu(v):
    return 0.5 * v * (1.0 + np.tanh(np.sqrt(2.0 / np.pi) * (v + 0.044715 * v**3)))


def bf(x):
    return np.asarray(x, np.float32).astype(ml_dtypes.bfloat16)


def planes(Y):
    n, m = Y.shape
    b = f64(bf(Y)).reshape(n // 32, 32, m)
    amax = np.abs(b).max(1)
    byte = np.clip(np.where(amax > 0, np.frexp(amax)[1] - 1 + 127 - 7, 1), 1, 254)
    codes = (b * np.exp2(127.0 - byte)[:, None, :]).reshape(n, m).astype(np.float32).astype(ml_dtypes.float8_e4m3fn).view(np.uint8)
    words = codes.reshape(n // 512, 128, 4, m).transpose(0, 1, 3, 2)
    return np.ascontiguousarray(words), np.ascontiguousarray(byte.astype(np.uint8).reshape(n // 512, 16, m))


K, K3, H, N, S, T, T2, T3 = 1024, 512, 1024, 1024, 512, 2048, 1024, 2048

def setup_inputs():
    n = np.random.standard_normal
    s = mx_kscale(K)[:, None]
    s3 = mx_kscale(K3)[:, None]
    u = mx_kscale(H)[:, None]
    size = np.exp(0.8 * n(N))[None, :]
    tab_words, tab_scales = pack_weight(n((K, T)) * s, "e4m3")
    tab2_words, tab2_scales = pack_weight(n((K, T2)) * s, "e4m3")
    tab3_words, tab3_scales = pack_weight(n((K3, T3)) * s3, "e2m1")
    w2_words, w2_scales = pack_weight(n((K, H)) / np.sqrt(K) / s, "e2m1")
    w4_words, w4_scales = pack_weight(n((H, N)) / np.sqrt(H) / u * size, "e4m3")
    return {
        "tab_words": tab_words, "tab_scales": tab_scales,
        "tab2_words": tab2_words, "tab2_scales": tab2_scales,
        "tab3_words": tab3_words, "tab3_scales": tab3_scales,
        "offs": striped(np.random.permutation(T)[:S]),
        "offs2": striped(np.random.permutation(T2)[:S]),
        "offs3": striped(np.random.permutation(T3)[:S]),
        "w1": (n((K, H)) / np.sqrt(K) / s * u.T).astype(np.float32),
        "w2_words": w2_words, "w2_scales": w2_scales,
        "w3": (n((K3, N)) / np.sqrt(K3) / s3 * size).astype(np.float32),
        "w4_words": w4_words, "w4_scales": w4_scales,
    }

def reference(tab_words, tab_scales, tab2_words, tab2_scales, tab3_words, tab3_scales, offs, offs2, offs3,
              w1, w2_words, w2_scales, w3, w4_words, w4_scales):
    v = unpack_weight(tab_words, tab_scales, "e4m3")[:, unstriped(offs)]
    v2 = unpack_weight(tab2_words, tab2_scales, "e4m3")[:, unstriped(offs2)]
    v3 = unpack_weight(tab3_words, tab3_scales, "e2m1")[:, unstriped(offs3)]
    a = mxq(f64(w1), 0, "e4m3").T @ v
    b = unpack_weight(w2_words, w2_scales, "e2m1").T @ v2
    z = a * b
    q = unpack_weight(w4_words, w4_scales, "e4m3").T @ mxq(z, 0, "e4m3")
    lim = np.abs(mxq(f64(w3), 0, "e4m3").T @ v3)
    y = np.maximum(np.minimum(q, lim), -lim)
    words, scales = planes(y)
    return y, words, scales

@@ -1,0 +1,319 @@
+from contextlib import ExitStack
+
+import concourse.mybir as mybir
+
+FLOPS = 3758096384
+
+F32 = mybir.dt.float32
+BF16 = mybir.dt.bfloat16
+I32 = mybir.dt.int32
+U32 = mybir.dt.uint32
+U16 = mybir.dt.uint16
+U8 = mybir.dt.uint8
+FP8X4 = mybir.dt.float8_e4m3fn_x4
+FP4X4 = mybir.dt.float4_e2m1fn_x4
+ALU = mybir.AluOpType
+ACT = mybir.ActivationFunctionType
+
+P = 128
+S = 512
+G = 512
+
+
+def tile_list_stamp_trade_limits_kernel(
+    tc, tab_words, tab_scales, tab2_words, tab2_scales, tab3_words, tab3_scales, offs, offs2, offs3,
+    w1, w2_words, w2_scales, w3, w4_words, w4_scales, out_0, out_1, out_2,
+):
+    nc = tc.nc
+    with ExitStack() as ctx:
+        keep = ctx.enter_context(tc.tile_pool(name="keep", bufs=1))
+        ring = ctx.enter_context(tc.tile_pool(name="ring", bufs=2))
+        psum = ctx.enter_context(tc.psum_pool(name="psum", bufs=4))
+
+        def held(name, shape, dtype):
+            return keep.tile(shape, dtype, name=name, align_bytes=64)
+
+        list1 = held("list1", [P, 32], U16)
+        list2 = held("list2", [P, 32], U16)
+        list3 = held("list3", [P, 32], U16)
+        t1w = [held("t1w%d" % a, [P, 2048], I32) for a in range(2)]
+        t2w = [held("t2w%d" % a, [P, 1024], I32) for a in range(2)]
+        t3w = held("t3w", [P, 2048], U16)
+        t1s = held("t1s", [P, 2048], U8)
+        t2s = held("t2s", [P, 1024], U8)
+        t3s = held("t3s", [P, 2048], U8)
+        ws = held("ws", [P, 1024], U8)
+        wsd = held("wsd", [P, 1024], U8)
+        w2s1 = held("w2s1", [P, 1024], U8)
+        v1w = [held("v1w%d" % a, [P, S], U32) for a in range(2)]
+        v2w = [held("v2w%d" % a, [P, S], U32) for a in range(2)]
+        v3w = held("v3w", [P, S], U16)
+        v1s = held("v1s", [P, S], U8)
+        v2s = held("v2s", [P, S], U8)
+        v2s1 = held("v2s1", [P, S], U8)
+        v3s = held("v3s", [P, S], U8)
+        w2r = held("w2r", [P, 2048], U16)
+        w2d = held("w2d", [P, 2048], U16)
+        w4r = [held("w4r%d" % g, [P, 1024], I32) for g in range(2)]
+        w4d = [held("w4d%d" % g, [P, 1024], I32) for g in range(2)]
+
+        warm = held("warm", [P, 8], F32)
+        warm2 = held("warm2", [P, 8], F32)
+        nc.gpsimd.memset(warm[:], 0.0)
+        nc.scalar.activation(out=warm2[:], in_=warm[:], func=ACT.Abs)
+
+        nc.vector.memset(t2s[:].bitcast(I32), 0)
+        nc.vector.memset(ws[:].bitcast(I32), 0)
+        nc.vector.memset(t1s[:].bitcast(I32), 0)
+        nc.vector.memset(t3s[:].bitcast(I32), 0)
+        nc.vector.memset(v2s1[:].bitcast(I32), 0)
+        nc.vector.memset(w2s1[:].bitcast(I32), 0)
+
+        def load_words(dst, src):
+            nc.sync.dma_start(out=dst, in_=src)
+
+        def words4(src):
+            return src.rearrange("p n i -> p (n i)").bitcast(I32)
+
+        def load_planes(queue, dst, row0, scales):
+            n = scales.shape[0]
+            for q in range(4):
+                queue.dma_start(
+                    out=dst[32 * q + row0 : 32 * q + row0 + 4 * n, :].bitcast(I32),
+                    in_=scales[:, 4 * q : 4 * q + 4, :].bitcast(I32),
+                )
+
+        raws = {}
+
+        def load_weight(key, rows, g, half):
+            raw = held("raw_%s_%d_%d" % (key, g, half), [P, 4, 256], F32)
+            c0 = G * g + 256 * half
+            nc.sync.dma_start(out=raw[:], in_=rows.rearrange("(p i) c -> p i c", i=4)[:, :, c0 : c0 + 256])
+            raws[(key, g, half)] = raw
+
+        w1a = [w1[0:512, :], w1[512:1024, :]]
+
+        load_planes(nc.gpsimd, t3s, 0, tab3_scales)
+
+        nc.sync.dma_start(list2[:], offs2)
+        load_words(t2w[0][:], words4(tab2_words[0]))
+        load_weight("w1a0", w1a[0], 0, 0)
+        load_planes(nc.sync, t2s, 0, tab2_scales)
+        load_weight("w1a0", w1a[0], 0, 1)
+        load_words(w2r[:].bitcast(I32).rearrange("p (a n) -> p a n", a=2), w2_words.rearrange("a p n -> p a n").bitcast(I32))
+        load_planes(nc.sync, ws, 0, w2_scales)
+        load_planes(nc.sync, ws, 8, w4_scales)
+        load_words(t2w[1][:], words4(tab2_words[1]))
+        nc.sync.dma_start(list1[:], offs)
+        load_weight("w1a1", w1a[1], 0, 0)
+        load_weight("w1a1", w1a[1], 0, 1)
+        load_planes(nc.sync, t1s, 0, tab_scales)
+        load_words(t1w[0][:], words4(tab_words[0]))
+        load_words(t1w[1][:], words4(tab_words[1]))
+        for a in range(2):
+            for half in range(2):
+                load_weight("w1a%d" % a, w1a[a], 1, half)
+        nc.sync.dma_start(list3[:], offs3)
+        w4v = w4_words.rearrange("a p n i -> p a (n i)").bitcast(I32)
+        for g in range(2):
+            load_weight("w3", w3, g, 0)
+            load_weight("w3", w3, g, 1)
+            if g == 0:
+                load_words(t3w[:].bitcast(I32), tab3_words[0].bitcast(I32))
+            load_words(w4r[g][:].rearrange("p (a n) -> p a n", a=2), w4v[:, :, G * g : G * g + G])
+
+        def gather(dst, window, lst):
+            nc.vector.tensor_copy(out=dst, in_=window.indirect(lst[:]))
+
+        def deal(dst, src, run):
+            nc.vector.tensor_copy(
+                out=dst.rearrange("p (g t b m) -> p g b t m", t=4, m=run, b=P // run),
+                in_=src.rearrange("p (g b m t) -> p g b t m", t=4, m=run, b=P // run),
+            )
+
+        grouped = {}
+        wq = {}
+
+        def cast_weight(key, g, half):
+            if half == 0:
+                grouped[(key, g)] = ring.tile([P, 2048], BF16, name="grouped", bufs=3, align_bytes=64)
+            dst = grouped[(key, g)][:].rearrange("p (t m i) -> p m i t", t=4, i=4)[:, 64 * half : 64 * half + 64]
+            nc.scalar.copy(out=dst, in_=raws[(key, g, half)][:].rearrange("p i (m t) -> p m i t", t=4))
+
+        def quantize_weight(key, g):
+            codes = held("c_%s_%d" % (key, g), [P, G], U32)
+            scales = held("s_%s_%d" % (key, g), [P, G], U8)
+            nc.vector.quantize_mx(out=codes[:].bitcast(FP8X4), scales=scales[:], in_=grouped[(key, g)][:])
+            wq[(key, g)] = (codes, scales)
+
+        b_sb = {}
+
+        def b_unit(g, c):
+            bank = psum.tile([P, 4, P], F32, name="bank_s")
+            js = slice(P * c, P * c + P)
+            for t in range(4):
+                col = G * g + P * t
+                for a in range(2):
+                    nc.tensor.matmul_mx(
+                        out=bank[:, t, :],
+                        lhsT=w2d[:, 1024 * a + col : 1024 * a + col + P].bitcast(FP4X4),
+                        lhsT_scale=(wsd, w2s1)[a][:, col : col + P],
+                        rhs=v2w[a][:, js].bitcast(FP8X4),
+                        rhs_scale=(v2s, v2s1)[a][:, js],
+                        start=(a == 0), stop=(a == 1),
+                    )
+            b = held("b_%d_%d" % (g, c), [P, P, 4], F32)
+            nc.scalar.copy(out=b[:], in_=bank[:].rearrange("p t j -> p j t"))
+            b_sb[(g, c)] = b
+
+        z_bf = {}
+        zq = {}
+
+        def a_unit(g, c):
+            bank = psum.tile([P, 4, P], F32, name="bank_v")
+            js = slice(P * c, P * c + P)
+            for t in range(4):
+                cols = slice(P * t, P * t + P)
+                for a in range(2):
+                    codes, scales = wq[("w1a%d" % a, g)]
+                    nc.tensor.matmul_mx(
+                        out=bank[:, t, :],
+                        lhsT=codes[:, cols].bitcast(FP8X4),
+                        lhsT_scale=scales[:, cols],
+                        rhs=v1w[a][:, js].bitcast(FP8X4),
+                        rhs_scale=v1s[4 * a :, js],
+                        start=(a == 0), stop=(a == 1),
+                    )
+            h, half = divmod(c, 2)
+            if half == 0:
+                z_bf[(g, h)] = held("z_%d_%d" % (g, h), [P, 256, 4], BF16)
+            nc.vector.tensor_tensor(
+                out=z_bf[(g, h)][:, P * half : P * half + P, :], in0=bank[:].rearrange("p t j -> p j t"),
+                in1=b_sb[(g, c)][:], op=ALU.mult,
+            )
+
+        def quantize_z(g, h):
+            codes = held("zc_%d_%d" % (g, h), [P, 256], U32)
+            scales = held("zs_%d_%d" % (g, h), [P, 256], U8)
+            nc.vector.quantize_mx(
+                out=codes[:].bitcast(FP8X4), scales=scales[:], in_=z_bf[(g, h)][:].rearrange("p j t -> p (j t)")
+            )
+            zq[(g, h)] = (codes, scales)
+
+        lim = [held("lim%d" % g, [P, 4, S], F32) for g in range(2)]
+
+        def lim_unit(g, t):
+            bank = psum.tile([P, S], F32, name="bank_s")
+            codes, scales = wq[("w3", g)]
+            cols = slice(P * t, P * t + P)
+            nc.tensor.matmul_mx(
+                out=bank[:], lhsT=codes[:, cols].bitcast(FP8X4), lhsT_scale=scales[:, cols],
+                rhs=v3w[:].bitcast(FP4X4), rhs_scale=v3s[:], start=True, stop=True,
+            )
+            nc.scalar.activation(out=lim[g][:, t, :], in_=bank[:], func=ACT.Abs)
+
+        y_codes = held("y_codes", [P, 2, S], I32)
+        y_scales = held("y_scales", [P, 2, S], U8)
+        out_rows = out_0.rearrange("(g p t) j -> g p t j", t=4, p=P)
+        y_bf = {}
+
+        def q_unit(g, h):
+            js = slice(256 * h, 256 * h + 256)
+            low = ring.tile([P, 4, 256], F32, name="low", align_bytes=64)
+            y = held("y_%d_%d" % (g, h), [P, 4, 256], F32)
+            for u in range(2):
+                bank = psum.tile([P, 2, 256], F32, name="bank_v")
+                for e in range(2):
+                    t = 2 * u + e
+                    for a in range(2):
+                        codes, scales = zq[(a, h)]
+                        nc.tensor.matmul_mx(
+                            out=bank[:, e, :],
+                            lhsT=w4d[g][:, G * a + P * t : G * a + P * t + P].bitcast(FP8X4),
+                            lhsT_scale=wsd[8 + 4 * a :, G * g + P * t : G * g + P * t + P],
+                            rhs=codes[:].bitcast(FP8X4), rhs_scale=scales[:],
+                            start=(a == 0), stop=(a == 1),
+                        )
+                ts = slice(2 * u, 2 * u + 2)
+                nc.vector.tensor_tensor(out=low[:, ts, :], in0=bank[:], in1=lim[g][:, ts, js], op=ALU.min)
+            for u in range(2):
+                ts = slice(2 * u, 2 * u + 2)
+                nc.vector.scalar_tensor_tensor(
+                    out=y[:, ts, :], in0=lim[g][:, ts, js], scalar=-1.0, in1=low[:, ts, :], op0=ALU.mult, op1=ALU.max
+                )
+            nc.sync.dma_start(out=out_rows[g][:, :, js], in_=y[:])
+            rounded = ring.tile([P, 256, 4], BF16, name="rounded", align_bytes=64)
+            nc.scalar.copy(
+                out=rounded[:].rearrange("p (c i) t -> p c t i", i=4), in_=y[:].rearrange("p t (c i) -> p c t i", i=4)
+            )
+            y_bf[(g, h)] = rounded
+
+        def planes(g, h):
+            js = slice(256 * h, 256 * h + 256)
+            nc.vector.quantize_mx(
+                out=y_codes[:, g, js].bitcast(FP8X4), scales=y_scales[:, g, js],
+                in_=y_bf[(g, h)][:].rearrange("p j t -> p (j t)"),
+            )
+            nc.sync.dma_start(out=words4(out_1[g])[:, js], in_=y_codes[:, g, js])
+
+        gather(v2w[0][:], t2w[0][:].bitcast(U32), list2)
+        cast_weight("w1a0", 0, 0)
+        gather(v2s[:], t2s[:], list2)
+        nc.sync.dma_start(out=v2s1[0:100, :].bitcast(I32), in_=v2s[4:104, :].bitcast(I32))
+        cast_weight("w1a0", 0, 1)
+        deal(wsd[:], ws[:], 16)
+        nc.sync.dma_start(out=w2s1[0:100, :].bitcast(I32), in_=wsd[4:104, :].bitcast(I32))
+        deal(w2d[:], w2r[:], 8)
+        gather(v2w[1][:], t2w[1][:].bitcast(U32), list2)
+        quantize_weight("w1a0", 0)
+        gather(v1s[:], t1s[:], list1)
+        cast_weight("w1a1", 0, 0)
+        cast_weight("w1a1", 0, 1)
+        for c in range(4):
+            b_unit(0, c)
+        gather(v1w[0][:], t1w[0][:].bitcast(U32), list1)
+        quantize_weight("w1a1", 0)
+        gather(v1w[1][:], t1w[1][:].bitcast(U32), list1)
+        for c in range(4):
+            b_unit(1, c)
+        cast_weight("w1a0", 1, 0)
+        cast_weight("w1a0", 1, 1)
+        for c in range(4):
+            a_unit(0, c)
+        cast_weight("w1a1", 1, 0)
+        cast_weight("w1a1", 1, 1)
+        quantize_weight("w1a0", 1)
+        quantize_z(0, 0)
+        quantize_z(0, 1)
+        gather(v3s[:], t3s[:], list3)
+        quantize_weight("w1a1", 1)
+        cast_weight("w3", 0, 0)
+        cast_weight("w3", 0, 1)
+        for c in range(4):
+            a_unit(1, c)
+        gather(v3w[:], t3w[:], list3)
+        quantize_z(1, 0)
+        quantize_weight("w3", 0)
+        quantize_z(1, 1)
+        deal(w4d[0][:], w4r[0][:], 4)
+        for t in range(4):
+            lim_unit(0, t)
+        cast_weight("w3", 1, 0)
+        cast_weight("w3", 1, 1)
+        q_unit(0, 0)
+        quantize_weight("w3", 1)
+        deal(w4d[1][:], w4r[1][:], 4)
+        for t in range(4):
+            lim_unit(1, t)
+        q_unit(0, 1)
+        planes(0, 0)
+        q_unit(1, 0)
+        planes(0, 1)
+        q_unit(1, 1)
+        planes(1, 0)
+        planes(1, 1)
+        for q in range(4):
+            nc.sync.dma_start(
+                out=out_2[:, 4 * q : 4 * q + 4, :].rearrange("g r j -> r g j").bitcast(I32),
+                in_=y_scales[32 * q : 32 * q + 4, :, :].bitcast(I32),
+            )

@@ -42,9 +42,8 @@ def tile_list_stamp_trade_limits_kernel(
         t1s = held("t1s", [P, 2048], U8)
         t2s = held("t2s", [P, 1024], U8)
         t3s = held("t3s", [P, 2048], U8)
-        ws = held("ws", [P, 1024], U8)
-        wsd = held("wsd", [P, 1024], U8)
-        w2s1 = held("w2s1", [P, 1024], U8)
+        ws = held("ws", [P, 2048], U8)
+        wsd = held("wsd", [P, 2048], U8)
         v1w = [held("v1w%d" % a, [P, S], U32) for a in range(2)]
         v2w = [held("v2w%d" % a, [P, S], U32) for a in range(2)]
         v3w = held("v3w", [P, S], U16)
@@ -59,15 +58,14 @@ def tile_list_stamp_trade_limits_kernel(
 
         warm = held("warm", [P, 8], F32)
         warm2 = held("warm2", [P, 8], F32)
-        nc.gpsimd.memset(warm[:], 0.0)
+        nc.gpsimd.memset(t2s[:].bitcast(I32), 0)
+        nc.gpsimd.memset(t1s[:].bitcast(I32), 0)
+        nc.vector.memset(warm[:], 0.0)
         nc.scalar.activation(out=warm2[:], in_=warm[:], func=ACT.Abs)
 
-        nc.vector.memset(t2s[:].bitcast(I32), 0)
         nc.vector.memset(ws[:].bitcast(I32), 0)
-        nc.vector.memset(t1s[:].bitcast(I32), 0)
-        nc.vector.memset(t3s[:].bitcast(I32), 0)
         nc.vector.memset(v2s1[:].bitcast(I32), 0)
-        nc.vector.memset(w2s1[:].bitcast(I32), 0)
+        nc.vector.memset(t3s[:].bitcast(I32), 0)
 
         def load_words(dst, src):
             nc.sync.dma_start(out=dst, in_=src)
@@ -83,44 +81,30 @@ def tile_list_stamp_trade_limits_kernel(
                     in_=scales[:, 4 * q : 4 * q + 4, :].bitcast(I32),
                 )
 
+        def load_weight_planes(row0, scales):
+            for q in range(4):
+                nc.sync.dma_start(
+                    out=ws[32 * q + row0 : 32 * q + row0 + 4, :].bitcast(I32).rearrange("r (a n) -> r a n", a=2),
+                    in_=scales[:, 4 * q : 4 * q + 4, :].rearrange("a r n -> r a n").bitcast(I32),
+                )
+
         raws = {}
 
         def load_weight(key, rows, g, half):
             raw = held("raw_%s_%d_%d" % (key, g, half), [P, 4, 256], F32)
             c0 = G * g + 256 * half
             nc.sync.dma_start(out=raw[:], in_=rows.rearrange("(p i) c -> p i c", i=4)[:, :, c0 : c0 + 256])
-            raws[(key, g, half)] = raw
+            raws[(key, g, half)] = raw[:]
+
+        def load_weight_whole(key, rows, g):
+            raw = held("raw_%s_%d" % (key, g), [P, 4, G], F32)
+            nc.sync.dma_start(out=raw[:], in_=rows.rearrange("(p i) c -> p i c", i=4)[:, :, G * g : G * g + G])
+            raws[(key, g, 0)] = raw[:, :, 0:256]
+            raws[(key, g, 1)] = raw[:, :, 256:512]
 
         w1a = [w1[0:512, :], w1[512:1024, :]]
 
-        load_planes(nc.gpsimd, t3s, 0, tab3_scales)
-
-        nc.sync.dma_start(list2[:], offs2)
-        load_words(t2w[0][:], words4(tab2_words[0]))
-        load_weight("w1a0", w1a[0], 0, 0)
-        load_planes(nc.sync, t2s, 0, tab2_scales)
-        load_weight("w1a0", w1a[0], 0, 1)
-        load_words(w2r[:].bitcast(I32).rearrange("p (a n) -> p a n", a=2), w2_words.rearrange("a p n -> p a n").bitcast(I32))
-        load_planes(nc.sync, ws, 0, w2_scales)
-        load_planes(nc.sync, ws, 8, w4_scales)
-        load_words(t2w[1][:], words4(tab2_words[1]))
-        nc.sync.dma_start(list1[:], offs)
-        load_weight("w1a1", w1a[1], 0, 0)
-        load_weight("w1a1", w1a[1], 0, 1)
-        load_planes(nc.sync, t1s, 0, tab_scales)
-        load_words(t1w[0][:], words4(tab_words[0]))
-        load_words(t1w[1][:], words4(tab_words[1]))
-        for a in range(2):
-            for half in range(2):
-                load_weight("w1a%d" % a, w1a[a], 1, half)
-        nc.sync.dma_start(list3[:], offs3)
         w4v = w4_words.rearrange("a p n i -> p a (n i)").bitcast(I32)
-        for g in range(2):
-            load_weight("w3", w3, g, 0)
-            load_weight("w3", w3, g, 1)
-            if g == 0:
-                load_words(t3w[:].bitcast(I32), tab3_words[0].bitcast(I32))
-            load_words(w4r[g][:].rearrange("p (a n) -> p a n", a=2), w4v[:, :, G * g : G * g + G])
 
         def gather(dst, window, lst):
             nc.vector.tensor_copy(out=dst, in_=window.indirect(lst[:]))
@@ -134,11 +118,11 @@ def tile_list_stamp_trade_limits_kernel(
         grouped = {}
         wq = {}
 
-        def cast_weight(key, g, half):
+        def cast_weight(key, g, half, copy):
             if half == 0:
                 grouped[(key, g)] = ring.tile([P, 2048], BF16, name="grouped", bufs=3, align_bytes=64)
-            dst = grouped[(key, g)][:].rearrange("p (t m i) -> p m i t", t=4, i=4)[:, 64 * half : 64 * half + 64]
-            nc.scalar.copy(out=dst, in_=raws[(key, g, half)][:].rearrange("p i (m t) -> p m i t", t=4))
+            dst = grouped[(key, g)][:].rearrange("p (t m i) -> p m t i", t=4, i=4)[:, 64 * half : 64 * half + 64]
+            copy(out=dst, in_=raws[(key, g, half)].rearrange("p i (m t) -> p m t i", t=4))
 
         def quantize_weight(key, g):
             codes = held("c_%s_%d" % (key, g), [P, G], U32)
@@ -157,7 +141,7 @@ def tile_list_stamp_trade_limits_kernel(
                     nc.tensor.matmul_mx(
                         out=bank[:, t, :],
                         lhsT=w2d[:, 1024 * a + col : 1024 * a + col + P].bitcast(FP4X4),
-                        lhsT_scale=(wsd, w2s1)[a][:, col : col + P],
+                        lhsT_scale=wsd[:, 1024 * a + col : 1024 * a + col + P],
                         rhs=v2w[a][:, js].bitcast(FP8X4),
                         rhs_scale=(v2s, v2s1)[a][:, js],
                         start=(a == 0), stop=(a == 1),
@@ -217,7 +201,7 @@ def tile_list_stamp_trade_limits_kernel(
         out_rows = out_0.rearrange("(g p t) j -> g p t j", t=4, p=P)
         y_bf = {}
 
-        def q_unit(g, h):
+        def q_unit(g, h, copy):
             js = slice(256 * h, 256 * h + 256)
             low = ring.tile([P, 4, 256], F32, name="low", align_bytes=64)
             y = held("y_%d_%d" % (g, h), [P, 4, 256], F32)
@@ -230,7 +214,7 @@ def tile_list_stamp_trade_limits_kernel(
                         nc.tensor.matmul_mx(
                             out=bank[:, e, :],
                             lhsT=w4d[g][:, G * a + P * t : G * a + P * t + P].bitcast(FP8X4),
-                            lhsT_scale=wsd[8 + 4 * a :, G * g + P * t : G * g + P * t + P],
+                            lhsT_scale=wsd[4:, 1024 * a + G * g + P * t : 1024 * a + G * g + P * t + P],
                             rhs=codes[:].bitcast(FP8X4), rhs_scale=scales[:],
                             start=(a == 0), stop=(a == 1),
                         )
@@ -243,7 +227,7 @@ def tile_list_stamp_trade_limits_kernel(
                 )
             nc.sync.dma_start(out=out_rows[g][:, :, js], in_=y[:])
             rounded = ring.tile([P, 256, 4], BF16, name="rounded", align_bytes=64)
-            nc.scalar.copy(
+            copy(
                 out=rounded[:].rearrange("p (c i) t -> p c t i", i=4), in_=y[:].rearrange("p t (c i) -> p c t i", i=4)
             )
             y_bf[(g, h)] = rounded
@@ -256,60 +240,100 @@ def tile_list_stamp_trade_limits_kernel(
             )
             nc.sync.dma_start(out=words4(out_1[g])[:, js], in_=y_codes[:, g, js])
 
-        gather(v2w[0][:], t2w[0][:].bitcast(U32), list2)
-        cast_weight("w1a0", 0, 0)
+        sc = nc.scalar.copy
+        vc = nc.vector.tensor_copy
+        nc.sync.dma_start(list2[:], offs2)
+        load_words(t2w[0][:], words4(tab2_words[0]))
+        load_planes(nc.sync, t2s, 0, tab2_scales)
+        load_words(w2r[:].bitcast(I32).rearrange("p (a n) -> p a n", a=2), w2_words.rearrange("a p n -> p a n").bitcast(I32))
+        load_weight("w1a0", w1a[0], 0, 0)
+        load_weight_planes(0, w2_scales)
+        load_words(t2w[1][:], words4(tab2_words[1]))
+        load_weight("w1a0", w1a[0], 0, 1)
+        load_weight_planes(4, w4_scales)
+        load_weight_whole("w1a1", w1a[1], 0)
         gather(v2s[:], t2s[:], list2)
         nc.sync.dma_start(out=v2s1[0:100, :].bitcast(I32), in_=v2s[4:104, :].bitcast(I32))
-        cast_weight("w1a0", 0, 1)
-        deal(wsd[:], ws[:], 16)
-        nc.sync.dma_start(out=w2s1[0:100, :].bitcast(I32), in_=wsd[4:104, :].bitcast(I32))
+        nc.sync.dma_start(list1[:], offs)
+        load_planes(nc.sync, t1s, 0, tab_scales)
+        load_words(t1w[0][:], words4(tab_words[0]))
+        nc.sync.dma_start(list3[:], offs3)
+        load_planes(nc.sync, t3s, 0, tab3_scales)
+        load_words(t1w[1][:], words4(tab_words[1]))
+        load_weight("w1a0", w1a[0], 1, 0)
+        load_weight("w1a0", w1a[0], 1, 1)
+        load_weight("w1a1", w1a[1], 1, 0)
+        load_weight("w1a1", w1a[1], 1, 1)
+        load_weight("w3", w3, 0, 0)
+        load_weight("w3", w3, 0, 1)
+        load_words(t3w[:].bitcast(I32), tab3_words[0].bitcast(I32))
+        load_words(w4r[0][:].rearrange("p (a n) -> p a n", a=2), w4v[:, :, G * 0 : G * 0 + G])
+        load_weight("w3", w3, 1, 0)
+        load_weight("w3", w3, 1, 1)
+        load_words(w4r[1][:].rearrange("p (a n) -> p a n", a=2), w4v[:, :, G * 1 : G * 1 + G])
+        gather(v2w[0][:], t2w[0][:].bitcast(U32), list2)
+        cast_weight("w1a0", 0, 0, sc)
         deal(w2d[:], w2r[:], 8)
         gather(v2w[1][:], t2w[1][:].bitcast(U32), list2)
-        quantize_weight("w1a0", 0)
         gather(v1s[:], t1s[:], list1)
-        cast_weight("w1a1", 0, 0)
-        cast_weight("w1a1", 0, 1)
-        for c in range(4):
-            b_unit(0, c)
+        deal(wsd[:], ws[:], 16)
+        cast_weight("w1a0", 0, 1, sc)
+        quantize_weight("w1a0", 0)
+        gather(v3s[:], t3s[:], list3)
+        b_unit(0, 0)
+        b_unit(0, 1)
+        b_unit(0, 2)
+        b_unit(0, 3)
+        cast_weight("w1a1", 0, 0, sc)
+        cast_weight("w1a1", 0, 1, sc)
+        b_unit(1, 0)
+        b_unit(1, 1)
+        b_unit(1, 2)
+        b_unit(1, 3)
         gather(v1w[0][:], t1w[0][:].bitcast(U32), list1)
         quantize_weight("w1a1", 0)
         gather(v1w[1][:], t1w[1][:].bitcast(U32), list1)
-        for c in range(4):
-            b_unit(1, c)
-        cast_weight("w1a0", 1, 0)
-        cast_weight("w1a0", 1, 1)
-        for c in range(4):
-            a_unit(0, c)
-        cast_weight("w1a1", 1, 0)
-        cast_weight("w1a1", 1, 1)
+        a_unit(0, 0)
+        a_unit(0, 1)
+        a_unit(0, 2)
+        a_unit(0, 3)
+        cast_weight("w1a0", 1, 0, sc)
+        cast_weight("w1a0", 1, 1, sc)
+        cast_weight("w1a1", 1, 0, vc)
+        cast_weight("w1a1", 1, 1, vc)
         quantize_weight("w1a0", 1)
+        quantize_weight("w1a1", 1)
         quantize_z(0, 0)
         quantize_z(0, 1)
-        gather(v3s[:], t3s[:], list3)
-        quantize_weight("w1a1", 1)
-        cast_weight("w3", 0, 0)
-        cast_weight("w3", 0, 1)
-        for c in range(4):
-            a_unit(1, c)
         gather(v3w[:], t3w[:], list3)
+        cast_weight("w3", 0, 0, sc)
+        cast_weight("w3", 0, 1, sc)
+        a_unit(1, 0)
+        a_unit(1, 1)
+        a_unit(1, 2)
         quantize_z(1, 0)
         quantize_weight("w3", 0)
-        quantize_z(1, 1)
+        a_unit(1, 3)
         deal(w4d[0][:], w4r[0][:], 4)
-        for t in range(4):
-            lim_unit(0, t)
-        cast_weight("w3", 1, 0)
-        cast_weight("w3", 1, 1)
-        q_unit(0, 0)
+        quantize_z(1, 1)
+        lim_unit(0, 0)
+        lim_unit(0, 1)
+        lim_unit(0, 2)
+        lim_unit(0, 3)
+        cast_weight("w3", 1, 0, sc)
+        cast_weight("w3", 1, 1, sc)
+        q_unit(0, 0, sc)
         quantize_weight("w3", 1)
         deal(w4d[1][:], w4r[1][:], 4)
-        for t in range(4):
-            lim_unit(1, t)
-        q_unit(0, 1)
+        lim_unit(1, 0)
+        lim_unit(1, 1)
+        lim_unit(1, 2)
+        lim_unit(1, 3)
+        q_unit(0, 1, sc)
         planes(0, 0)
-        q_unit(1, 0)
+        q_unit(1, 0, sc)
         planes(0, 1)
-        q_unit(1, 1)
+        q_unit(1, 1, vc)
         planes(1, 0)
         planes(1, 1)
         for q in range(4):

@@ -81,11 +81,12 @@ def tile_list_stamp_trade_limits_kernel(
                     in_=scales[:, 4 * q : 4 * q + 4, :].bitcast(I32),
                 )
 
-        def load_weight_planes(row0, scales):
-            for q in range(4):
+        def load_rows(dst, row0, scales):
+            n = scales.shape[0]
+            for r in range(4):
                 nc.sync.dma_start(
-                    out=ws[32 * q + row0 : 32 * q + row0 + 4, :].bitcast(I32).rearrange("r (a n) -> r a n", a=2),
-                    in_=scales[:, 4 * q : 4 * q + 4, :].rearrange("a r n -> r a n").bitcast(I32),
+                    out=dst[row0 + r : P : 32, :].bitcast(I32).rearrange("q (a n) -> q a n", a=n),
+                    in_=scales[:, r:16:4, :].rearrange("a q n -> q a n").bitcast(I32),
                 )
 
         raws = {}
@@ -146,8 +147,8 @@ def tile_list_stamp_trade_limits_kernel(
                         rhs_scale=(v2s, v2s1)[a][:, js],
                         start=(a == 0), stop=(a == 1),
                     )
-            b = held("b_%d_%d" % (g, c), [P, P, 4], F32)
-            nc.scalar.copy(out=b[:], in_=bank[:].rearrange("p t j -> p j t"))
+            b = held("b_%d_%d" % (g, c), [P, 64, 4, 2], F32)
+            nc.scalar.copy(out=b[:], in_=bank[:].rearrange("p t (j e) -> p j t e", e=2))
             b_sb[(g, c)] = b
 
         z_bf = {}
@@ -172,8 +173,8 @@ def tile_list_stamp_trade_limits_kernel(
             if half == 0:
                 z_bf[(g, h)] = held("z_%d_%d" % (g, h), [P, 256, 4], BF16)
             nc.vector.tensor_tensor(
-                out=z_bf[(g, h)][:, P * half : P * half + P, :], in0=bank[:].rearrange("p t j -> p j t"),
-                in1=b_sb[(g, c)][:], op=ALU.mult,
+                out=z_bf[(g, h)][:, P * half : P * half + P, :].rearrange("p (j e) t -> p j t e", e=2),
+                in0=bank[:].rearrange("p t (j e) -> p j t e", e=2), in1=b_sb[(g, c)][:], op=ALU.mult,
             )
 
         def quantize_z(g, h):
@@ -201,7 +202,7 @@ def tile_list_stamp_trade_limits_kernel(
         out_rows = out_0.rearrange("(g p t) j -> g p t j", t=4, p=P)
         y_bf = {}
 
-        def q_unit(g, h, copy):
+        def q_unit(g, h, copy, split=False):
             js = slice(256 * h, 256 * h + 256)
             low = ring.tile([P, 4, 256], F32, name="low", align_bytes=64)
             y = held("y_%d_%d" % (g, h), [P, 4, 256], F32)
@@ -225,7 +226,10 @@ def tile_list_stamp_trade_limits_kernel(
                 nc.vector.scalar_tensor_tensor(
                     out=y[:, ts, :], in0=lim[g][:, ts, js], scalar=-1.0, in1=low[:, ts, :], op0=ALU.mult, op1=ALU.max
                 )
-            nc.sync.dma_start(out=out_rows[g][:, :, js], in_=y[:])
+                if split:
+                    nc.sync.dma_start(out=out_rows[g][:, ts, js], in_=y[:, ts, :])
+            if not split:
+                nc.sync.dma_start(out=out_rows[g][:, :, js], in_=y[:])
             rounded = ring.tile([P, 256, 4], BF16, name="rounded", align_bytes=64)
             copy(
                 out=rounded[:].rearrange("p (c i) t -> p c t i", i=4), in_=y[:].rearrange("p t (c i) -> p c t i", i=4)
@@ -247,10 +251,10 @@ def tile_list_stamp_trade_limits_kernel(
         load_planes(nc.sync, t2s, 0, tab2_scales)
         load_words(w2r[:].bitcast(I32).rearrange("p (a n) -> p a n", a=2), w2_words.rearrange("a p n -> p a n").bitcast(I32))
         load_weight("w1a0", w1a[0], 0, 0)
-        load_weight_planes(0, w2_scales)
+        load_rows(ws, 0, w2_scales)
         load_words(t2w[1][:], words4(tab2_words[1]))
         load_weight("w1a0", w1a[0], 0, 1)
-        load_weight_planes(4, w4_scales)
+        load_rows(ws, 4, w4_scales)
         load_weight_whole("w1a1", w1a[1], 0)
         gather(v2s[:], t2s[:], list2)
         nc.sync.dma_start(out=v2s1[0:100, :].bitcast(I32), in_=v2s[4:104, :].bitcast(I32))
@@ -258,7 +262,7 @@ def tile_list_stamp_trade_limits_kernel(
         load_planes(nc.sync, t1s, 0, tab_scales)
         load_words(t1w[0][:], words4(tab_words[0]))
         nc.sync.dma_start(list3[:], offs3)
-        load_planes(nc.sync, t3s, 0, tab3_scales)
+        load_rows(t3s, 0, tab3_scales)
         load_words(t1w[1][:], words4(tab_words[1]))
         load_weight("w1a0", w1a[0], 1, 0)
         load_weight("w1a0", w1a[0], 1, 1)
@@ -299,8 +303,8 @@ def tile_list_stamp_trade_limits_kernel(
         a_unit(0, 3)
         cast_weight("w1a0", 1, 0, sc)
         cast_weight("w1a0", 1, 1, sc)
-        cast_weight("w1a1", 1, 0, vc)
-        cast_weight("w1a1", 1, 1, vc)
+        cast_weight("w1a1", 1, 0, sc)
+        cast_weight("w1a1", 1, 1, sc)
         quantize_weight("w1a0", 1)
         quantize_weight("w1a1", 1)
         quantize_z(0, 0)
@@ -333,11 +337,11 @@ def tile_list_stamp_trade_limits_kernel(
         planes(0, 0)
         q_unit(1, 0, sc)
         planes(0, 1)
-        q_unit(1, 1, vc)
+        q_unit(1, 1, vc, True)
         planes(1, 0)
         planes(1, 1)
-        for q in range(4):
+        for r in range(4):
             nc.sync.dma_start(
-                out=out_2[:, 4 * q : 4 * q + 4, :].rearrange("g r j -> r g j").bitcast(I32),
-                in_=y_scales[32 * q : 32 * q + 4, :, :].bitcast(I32),
+                out=out_2[:, r:16:4, :].rearrange("g q j -> q g j").bitcast(I32),
+                in_=y_scales[r:P:32, :, :].bitcast(I32),
             )

@@ -27,321 +27,317 @@ def tile_list_stamp_trade_limits_kernel(
     nc = tc.nc
     with ExitStack() as ctx:
         keep = ctx.enter_context(tc.tile_pool(name="keep", bufs=1))
-        ring = ctx.enter_context(tc.tile_pool(name="ring", bufs=2))
-        psum = ctx.enter_context(tc.psum_pool(name="psum", bufs=4))
+        psum = ctx.enter_context(tc.psum_pool(name="psum", bufs=1))
 
-        def held(name, shape, dtype):
-            return keep.tile(shape, dtype, name=name, align_bytes=64)
+        sb = {}
 
-        list1 = held("list1", [P, 32], U16)
-        list2 = held("list2", [P, 32], U16)
-        list3 = held("list3", [P, 32], U16)
-        t1w = [held("t1w%d" % a, [P, 2048], I32) for a in range(2)]
-        t2w = [held("t2w%d" % a, [P, 1024], I32) for a in range(2)]
-        t3w = held("t3w", [P, 2048], U16)
-        t1s = held("t1s", [P, 2048], U8)
-        t2s = held("t2s", [P, 1024], U8)
-        t3s = held("t3s", [P, 2048], U8)
-        ws = held("ws", [P, 2048], U8)
-        wsd = held("wsd", [P, 2048], U8)
-        v1w = [held("v1w%d" % a, [P, S], U32) for a in range(2)]
-        v2w = [held("v2w%d" % a, [P, S], U32) for a in range(2)]
-        v3w = held("v3w", [P, S], U16)
-        v1s = held("v1s", [P, S], U8)
-        v2s = held("v2s", [P, S], U8)
-        v2s1 = held("v2s1", [P, S], U8)
-        v3s = held("v3s", [P, S], U8)
-        w2r = held("w2r", [P, 2048], U16)
-        w2d = held("w2d", [P, 2048], U16)
-        w4r = [held("w4r%d" % g, [P, 1024], I32) for g in range(2)]
-        w4d = [held("w4d%d" % g, [P, 1024], I32) for g in range(2)]
-
-        warm = held("warm", [P, 8], F32)
-        warm2 = held("warm2", [P, 8], F32)
-        nc.gpsimd.memset(t2s[:].bitcast(I32), 0)
-        nc.gpsimd.memset(t1s[:].bitcast(I32), 0)
-        nc.vector.memset(warm[:], 0.0)
-        nc.scalar.activation(out=warm2[:], in_=warm[:], func=ACT.Abs)
-
-        nc.vector.memset(ws[:].bitcast(I32), 0)
-        nc.vector.memset(v2s1[:].bitcast(I32), 0)
-        nc.vector.memset(t3s[:].bitcast(I32), 0)
-
-        def load_words(dst, src):
-            nc.sync.dma_start(out=dst, in_=src)
+        def held(name, shape, dtype, over=None):
+            sb[name] = keep.tile(shape, dtype, name=name, tag=over or name, align_bytes=64)
+            return sb[name]
 
         def words4(src):
             return src.rearrange("p n i -> p (n i)").bitcast(I32)
 
-        def load_planes(queue, dst, row0, scales):
+        def load_list(name, src):
+            nc.sync.dma_start(held(name, [P, 32], U16)[:], src)
+
+        def load_table(name, src):
+            nc.sync.dma_start(out=held(name, [P, src.shape[1]], I32)[:], in_=words4(src))
+
+        def load_t3w():
+            nc.sync.dma_start(out=held("t3w", [P, 2048], U16)[:].bitcast(I32), in_=tab3_words[0].bitcast(I32))
+
+        def load_w2():
+            nc.sync.dma_start(
+                out=held("w2r", [P, 2048], U16)[:].bitcast(I32).rearrange("p (a n) -> p a n", a=2),
+                in_=w2_words.rearrange("a p n -> p a n").bitcast(I32),
+            )
+
+        def load_w4(g):
+            nc.sync.dma_start(
+                out=held("w4r%d" % g, [P, 1024], I32)[:].rearrange("p (a n) -> p a n", a=2),
+                in_=w4_words.rearrange("a p n i -> p a (n i)").bitcast(I32)[:, :, G * g : G * g + G],
+            )
+
+        def cleared(engine, name, width):
+            engine.memset(held(name, [P, width], U8)[:].bitcast(I32), 0)
+
+        def load_stacked(name, row0, scales, queue=nc.sync):
             n = scales.shape[0]
             for q in range(4):
                 queue.dma_start(
-                    out=dst[32 * q + row0 : 32 * q + row0 + 4 * n, :].bitcast(I32),
+                    out=sb[name][32 * q + row0 : 32 * q + row0 + 4 * n, :].bitcast(I32),
                     in_=scales[:, 4 * q : 4 * q + 4, :].bitcast(I32),
                 )
 
-        def load_rows(dst, row0, scales):
+        def load_beside(name, row0, scales, queue=nc.sync):
             n = scales.shape[0]
             for r in range(4):
-                nc.sync.dma_start(
-                    out=dst[row0 + r : P : 32, :].bitcast(I32).rearrange("q (a n) -> q a n", a=n),
+                queue.dma_start(
+                    out=sb[name][row0 + r : P : 32, :].bitcast(I32).rearrange("q (a n) -> q a n", a=n),
                     in_=scales[:, r:16:4, :].rearrange("a q n -> q a n").bitcast(I32),
                 )
 
-        raws = {}
-
-        def load_weight(key, rows, g, half):
-            raw = held("raw_%s_%d_%d" % (key, g, half), [P, 4, 256], F32)
-            c0 = G * g + 256 * half
-            nc.sync.dma_start(out=raw[:], in_=rows.rearrange("(p i) c -> p i c", i=4)[:, :, c0 : c0 + 256])
-            raws[(key, g, half)] = raw[:]
-
-        def load_weight_whole(key, rows, g):
-            raw = held("raw_%s_%d" % (key, g), [P, 4, G], F32)
-            nc.sync.dma_start(out=raw[:], in_=rows.rearrange("(p i) c -> p i c", i=4)[:, :, G * g : G * g + G])
-            raws[(key, g, 0)] = raw[:, :, 0:256]
-            raws[(key, g, 1)] = raw[:, :, 256:512]
-
-        w1a = [w1[0:512, :], w1[512:1024, :]]
-
-        w4v = w4_words.rearrange("a p n i -> p a (n i)").bitcast(I32)
-
-        def gather(dst, window, lst):
-            nc.vector.tensor_copy(out=dst, in_=window.indirect(lst[:]))
-
-        def deal(dst, src, run):
-            nc.vector.tensor_copy(
-                out=dst.rearrange("p (g t b m) -> p g b t m", t=4, m=run, b=P // run),
-                in_=src.rearrange("p (g b m t) -> p g b t m", t=4, m=run, b=P // run),
+        def load_weight(name, rows, g, c0=0, c1=G):
+            nc.sync.dma_start(
+                out=held("raw_" + name, [P, 4, c1 - c0], F32)[:],
+                in_=rows.rearrange("(p i) c -> p i c", i=4)[:, :, G * g + c0 : G * g + c1],
             )
 
-        grouped = {}
-        wq = {}
+        def gather(name, dtype, window, lst, over=None):
+            nc.vector.tensor_copy(out=held(name, [P, S], dtype, over)[:], in_=window.indirect(sb[lst][:]))
 
-        def cast_weight(key, g, half, copy):
-            if half == 0:
-                grouped[(key, g)] = ring.tile([P, 2048], BF16, name="grouped", bufs=3, align_bytes=64)
-            dst = grouped[(key, g)][:].rearrange("p (t m i) -> p m t i", t=4, i=4)[:, 64 * half : 64 * half + 64]
-            copy(out=dst, in_=raws[(key, g, half)].rearrange("p i (m t) -> p m t i", t=4))
+        def deal(name, src, run, over=None):
+            dst = held(name, list(sb[src].shape), sb[src].dtype, over)
+            nc.vector.tensor_copy(
+                out=dst[:].rearrange("p (g t b m) -> p g b t m", t=4, m=run, b=P // run),
+                in_=sb[src][:].rearrange("p (g b m t) -> p g b t m", t=4, m=run, b=P // run),
+            )
 
-        def quantize_weight(key, g):
-            codes = held("c_%s_%d" % (key, g), [P, G], U32)
-            scales = held("s_%s_%d" % (key, g), [P, G], U8)
-            nc.vector.quantize_mx(out=codes[:].bitcast(FP8X4), scales=scales[:], in_=grouped[(key, g)][:])
-            wq[(key, g)] = (codes, scales)
+        def cast_weight(name, copy, m0=0, m1=P, src=None, base=0, over=None):
+            if "bf_" + name not in sb:
+                held("bf_" + name, [P, 2048], BF16, over)
+            copy(
+                out=sb["bf_" + name][:].rearrange("p (t m i) -> p m i t", t=4, i=4)[:, m0:m1],
+                in_=sb["raw_" + (src or name)][:].rearrange("p i (m t) -> p m i t", t=4)[:, m0 - base : m1 - base],
+            )
 
-        b_sb = {}
+        def quantize(name, c0=0, c1=G, over=None):
+            if c0 == 0:
+                held("c_" + name, [P, G], U32, over)
+                held("s_" + name, [P, G], U8)
+            nc.vector.quantize_mx(
+                out=sb["c_" + name][:, c0:c1].bitcast(FP8X4), scales=sb["s_" + name][:, c0:c1],
+                in_=sb["bf_" + name][:, 4 * c0 : 4 * c1],
+            )
 
-        def b_unit(g, c):
-            bank = psum.tile([P, 4, P], F32, name="bank_s")
+        banks = {}
+
+        def opened(key, index, shape):
+            banks[key] = psum.tile(shape, F32, name="bank%d" % index)
+
+        def b_pass(g, c, a):
+            if a == 0:
+                opened(("b", g, c), 4 * g + c, [P, 4, P])
             js = slice(P * c, P * c + P)
             for t in range(4):
-                col = G * g + P * t
-                for a in range(2):
-                    nc.tensor.matmul_mx(
-                        out=bank[:, t, :],
-                        lhsT=w2d[:, 1024 * a + col : 1024 * a + col + P].bitcast(FP4X4),
-                        lhsT_scale=wsd[:, 1024 * a + col : 1024 * a + col + P],
-                        rhs=v2w[a][:, js].bitcast(FP8X4),
-                        rhs_scale=(v2s, v2s1)[a][:, js],
-                        start=(a == 0), stop=(a == 1),
-                    )
-            b = held("b_%d_%d" % (g, c), [P, 64, 4, 2], F32)
-            nc.scalar.copy(out=b[:], in_=bank[:].rearrange("p t (j e) -> p j t e", e=2))
-            b_sb[(g, c)] = b
+                cols = slice(1024 * a + G * g + P * t, 1024 * a + G * g + P * t + P)
+                nc.tensor.matmul_mx(
+                    out=banks[("b", g, c)][:, t, :],
+                    lhsT=sb["w2d"][:, cols].bitcast(FP4X4), lhsT_scale=sb["w2sd"][:, cols],
+                    rhs=sb["v2w%d" % a][:, js].bitcast(FP8X4), rhs_scale=sb["v2s%d" % a][:, js],
+                    start=(a == 0 and t == 0), stop=(a == 1 and t == 3),
+                )
 
-        z_bf = {}
-        zq = {}
+        def park_b(g, c, over=None):
+            if g == 0 and c == 0:
+                held("b", [P, 2, 4, 64, 4, 2], F32, over)
+            nc.scalar.copy(out=sb["b"][:, g, c], in_=banks[("b", g, c)][:].rearrange("p t (j e) -> p j t e", e=2))
 
-        def a_unit(g, c):
-            bank = psum.tile([P, 4, P], F32, name="bank_v")
+        def a_pass(g, c, a):
+            if a == 0:
+                opened(("a", g, c), 4 * g + c, [P, 4, P])
             js = slice(P * c, P * c + P)
             for t in range(4):
                 cols = slice(P * t, P * t + P)
-                for a in range(2):
-                    codes, scales = wq[("w1a%d" % a, g)]
-                    nc.tensor.matmul_mx(
-                        out=bank[:, t, :],
-                        lhsT=codes[:, cols].bitcast(FP8X4),
-                        lhsT_scale=scales[:, cols],
-                        rhs=v1w[a][:, js].bitcast(FP8X4),
-                        rhs_scale=v1s[4 * a :, js],
-                        start=(a == 0), stop=(a == 1),
-                    )
-            h, half = divmod(c, 2)
-            if half == 0:
-                z_bf[(g, h)] = held("z_%d_%d" % (g, h), [P, 256, 4], BF16)
+                nc.tensor.matmul_mx(
+                    out=banks[("a", g, c)][:, t, :],
+                    lhsT=sb["c_w1_%d%d" % (a, g)][:, cols].bitcast(FP8X4),
+                    lhsT_scale=sb["s_w1_%d%d" % (a, g)][:, cols],
+                    rhs=sb["v1w%d" % a][:, js].bitcast(FP8X4), rhs_scale=sb["v1s"][4 + 4 * a :, js],
+                    start=(a == 0 and t == 0), stop=(a == 1 and t == 3),
+                )
+
+        def product(g, c, over=None):
+            if c == 0:
+                held("bf_z%d" % g, [P, 2048], BF16, over)
             nc.vector.tensor_tensor(
-                out=z_bf[(g, h)][:, P * half : P * half + P, :].rearrange("p (j e) t -> p j t e", e=2),
-                in0=bank[:].rearrange("p t (j e) -> p j t e", e=2), in1=b_sb[(g, c)][:], op=ALU.mult,
+                out=sb["bf_z%d" % g][:, G * c : G * c + G].rearrange("p (j e t) -> p j t e", e=2, t=4),
+                in0=banks[("a", g, c)][:].rearrange("p t (j e) -> p j t e", e=2), in1=sb["b"][:, g, c], op=ALU.mult,
             )
 
-        def quantize_z(g, h):
-            codes = held("zc_%d_%d" % (g, h), [P, 256], U32)
-            scales = held("zs_%d_%d" % (g, h), [P, 256], U8)
-            nc.vector.quantize_mx(
-                out=codes[:].bitcast(FP8X4), scales=scales[:], in_=z_bf[(g, h)][:].rearrange("p j t -> p (j t)")
-            )
-            zq[(g, h)] = (codes, scales)
+        def lim_unit(g, h, u, over=None):
+            opened(("lim", g, h, u), 2 * h + u, [P, 2, 256])
+            bank = banks[("lim", g, h, u)]
+            js = slice(256 * h, 256 * h + 256)
+            for e in range(2):
+                cols = slice(P * (2 * u + e), P * (2 * u + e) + P)
+                nc.tensor.matmul_mx(
+                    out=bank[:, e, :],
+                    lhsT=sb["c_w3_%d" % g][:, cols].bitcast(FP8X4), lhsT_scale=sb["s_w3_%d" % g][:, cols],
+                    rhs=sb["v3w"][:, js].bitcast(FP4X4), rhs_scale=sb["v3s"][:, js], start=True, stop=True,
+                )
+            if u == 0:
+                held("lim%d%d" % (g, h), [P, 4, 256], F32, over)
+            nc.scalar.activation(out=sb["lim%d%d" % (g, h)][:, 2 * u : 2 * u + 2, :], in_=bank[:], func=ACT.Abs)
 
-        lim = [held("lim%d" % g, [P, 4, S], F32) for g in range(2)]
-
-        def lim_unit(g, t):
-            bank = psum.tile([P, S], F32, name="bank_s")
-            codes, scales = wq[("w3", g)]
-            cols = slice(P * t, P * t + P)
-            nc.tensor.matmul_mx(
-                out=bank[:], lhsT=codes[:, cols].bitcast(FP8X4), lhsT_scale=scales[:, cols],
-                rhs=v3w[:].bitcast(FP4X4), rhs_scale=v3s[:], start=True, stop=True,
-            )
-            nc.scalar.activation(out=lim[g][:, t, :], in_=bank[:], func=ACT.Abs)
+        def q_pass(g, h, u, a):
+            if a == 0:
+                opened(("q", g, h, u), 4 + 2 * h + u, [P, 2, 256])
+            js = slice(256 * h, 256 * h + 256)
+            for e in range(2):
+                t = 2 * u + e
+                nc.tensor.matmul_mx(
+                    out=banks[("q", g, h, u)][:, e, :],
+                    lhsT=sb["w4d%d" % g][:, G * a + P * t : G * a + P * t + P].bitcast(FP8X4),
+                    lhsT_scale=sb["w4sd"][8 + 4 * a :, G * g + P * t : G * g + P * t + P],
+                    rhs=sb["c_z%d" % a][:, js].bitcast(FP8X4), rhs_scale=sb["s_z%d" % a][:, js],
+                    start=(a == 0 and e == 0), stop=(a == 1 and e == 1),
+                )
 
         y_codes = held("y_codes", [P, 2, S], I32)
         y_scales = held("y_scales", [P, 2, S], U8)
         out_rows = out_0.rearrange("(g p t) j -> g p t j", t=4, p=P)
-        y_bf = {}
 
-        def q_unit(g, h, copy, split=False):
-            js = slice(256 * h, 256 * h + 256)
-            low = ring.tile([P, 4, 256], F32, name="low", align_bytes=64)
-            y = held("y_%d_%d" % (g, h), [P, 4, 256], F32)
-            for u in range(2):
-                bank = psum.tile([P, 2, 256], F32, name="bank_v")
-                for e in range(2):
-                    t = 2 * u + e
-                    for a in range(2):
-                        codes, scales = zq[(a, h)]
-                        nc.tensor.matmul_mx(
-                            out=bank[:, e, :],
-                            lhsT=w4d[g][:, G * a + P * t : G * a + P * t + P].bitcast(FP8X4),
-                            lhsT_scale=wsd[4:, 1024 * a + G * g + P * t : 1024 * a + G * g + P * t + P],
-                            rhs=codes[:].bitcast(FP8X4), rhs_scale=scales[:],
-                            start=(a == 0), stop=(a == 1),
-                        )
-                ts = slice(2 * u, 2 * u + 2)
-                nc.vector.tensor_tensor(out=low[:, ts, :], in0=bank[:], in1=lim[g][:, ts, js], op=ALU.min)
-            for u in range(2):
-                ts = slice(2 * u, 2 * u + 2)
-                nc.vector.scalar_tensor_tensor(
-                    out=y[:, ts, :], in0=lim[g][:, ts, js], scalar=-1.0, in1=low[:, ts, :], op0=ALU.mult, op1=ALU.max
-                )
-                if split:
-                    nc.sync.dma_start(out=out_rows[g][:, ts, js], in_=y[:, ts, :])
-            if not split:
-                nc.sync.dma_start(out=out_rows[g][:, :, js], in_=y[:])
-            rounded = ring.tile([P, 256, 4], BF16, name="rounded", align_bytes=64)
-            copy(
-                out=rounded[:].rearrange("p (c i) t -> p c t i", i=4), in_=y[:].rearrange("p t (c i) -> p c t i", i=4)
+        def q_min(g, h, u, over=None):
+            if u == 0:
+                held("low%d%d" % (g, h), [P, 4, 256], F32, over)
+            ts = slice(2 * u, 2 * u + 2)
+            nc.vector.tensor_tensor(
+                out=sb["low%d%d" % (g, h)][:, ts, :], in0=banks[("q", g, h, u)][:], in1=sb["lim%d%d" % (g, h)][:, ts, :],
+                op=ALU.min,
             )
-            y_bf[(g, h)] = rounded
+
+        def q_max(g, h, ts=slice(0, 4), over=None):
+            if ts.start == 0:
+                held("y%d%d" % (g, h), [P, 4, 256], F32, over)
+            nc.vector.scalar_tensor_tensor(
+                out=sb["y%d%d" % (g, h)][:, ts, :], in0=sb["lim%d%d" % (g, h)][:, ts, :], scalar=-1.0,
+                in1=sb["low%d%d" % (g, h)][:, ts, :], op0=ALU.mult, op1=ALU.max,
+            )
+            nc.sync.dma_start(out=out_rows[g][:, ts, 256 * h : 256 * h + 256], in_=sb["y%d%d" % (g, h)][:, ts, :])
+
+        def round_y(g, h, copy, over=None):
+            copy(
+                out=held("bf_y%d%d" % (g, h), [P, 256, 4], BF16, over)[:].rearrange("p (c i) t -> p c t i", i=4),
+                in_=sb["y%d%d" % (g, h)][:].rearrange("p t (c i) -> p c t i", i=4),
+            )
 
         def planes(g, h):
             js = slice(256 * h, 256 * h + 256)
             nc.vector.quantize_mx(
                 out=y_codes[:, g, js].bitcast(FP8X4), scales=y_scales[:, g, js],
-                in_=y_bf[(g, h)][:].rearrange("p j t -> p (j t)"),
+                in_=sb["bf_y%d%d" % (g, h)][:].rearrange("p j t -> p (j t)"),
             )
             nc.sync.dma_start(out=words4(out_1[g])[:, js], in_=y_codes[:, g, js])
 
+        def store_scales():
+            for r in range(4):
+                nc.sync.dma_start(
+                    out=out_2[:, r:16:4, :].rearrange("g q j -> q g j").bitcast(I32),
+                    in_=y_scales[r:P:32, :, :].bitcast(I32),
+                )
+
         sc = nc.scalar.copy
         vc = nc.vector.tensor_copy
-        nc.sync.dma_start(list2[:], offs2)
-        load_words(t2w[0][:], words4(tab2_words[0]))
-        load_planes(nc.sync, t2s, 0, tab2_scales)
-        load_words(w2r[:].bitcast(I32).rearrange("p (a n) -> p a n", a=2), w2_words.rearrange("a p n -> p a n").bitcast(I32))
-        load_weight("w1a0", w1a[0], 0, 0)
-        load_rows(ws, 0, w2_scales)
-        load_words(t2w[1][:], words4(tab2_words[1]))
-        load_weight("w1a0", w1a[0], 0, 1)
-        load_rows(ws, 4, w4_scales)
-        load_weight_whole("w1a1", w1a[1], 0)
-        gather(v2s[:], t2s[:], list2)
-        nc.sync.dma_start(out=v2s1[0:100, :].bitcast(I32), in_=v2s[4:104, :].bitcast(I32))
-        nc.sync.dma_start(list1[:], offs)
-        load_planes(nc.sync, t1s, 0, tab_scales)
-        load_words(t1w[0][:], words4(tab_words[0]))
-        nc.sync.dma_start(list3[:], offs3)
-        load_rows(t3s, 0, tab3_scales)
-        load_words(t1w[1][:], words4(tab_words[1]))
-        load_weight("w1a0", w1a[0], 1, 0)
-        load_weight("w1a0", w1a[0], 1, 1)
-        load_weight("w1a1", w1a[1], 1, 0)
-        load_weight("w1a1", w1a[1], 1, 1)
-        load_weight("w3", w3, 0, 0)
-        load_weight("w3", w3, 0, 1)
-        load_words(t3w[:].bitcast(I32), tab3_words[0].bitcast(I32))
-        load_words(w4r[0][:].rearrange("p (a n) -> p a n", a=2), w4v[:, :, G * 0 : G * 0 + G])
-        load_weight("w3", w3, 1, 0)
-        load_weight("w3", w3, 1, 1)
-        load_words(w4r[1][:].rearrange("p (a n) -> p a n", a=2), w4v[:, :, G * 1 : G * 1 + G])
-        gather(v2w[0][:], t2w[0][:].bitcast(U32), list2)
-        cast_weight("w1a0", 0, 0, sc)
-        deal(w2d[:], w2r[:], 8)
-        gather(v2w[1][:], t2w[1][:].bitcast(U32), list2)
-        gather(v1s[:], t1s[:], list1)
-        deal(wsd[:], ws[:], 16)
-        cast_weight("w1a0", 0, 1, sc)
-        quantize_weight("w1a0", 0)
-        gather(v3s[:], t3s[:], list3)
-        b_unit(0, 0)
-        b_unit(0, 1)
-        b_unit(0, 2)
-        b_unit(0, 3)
-        cast_weight("w1a1", 0, 0, sc)
-        cast_weight("w1a1", 0, 1, sc)
-        b_unit(1, 0)
-        b_unit(1, 1)
-        b_unit(1, 2)
-        b_unit(1, 3)
-        gather(v1w[0][:], t1w[0][:].bitcast(U32), list1)
-        quantize_weight("w1a1", 0)
-        gather(v1w[1][:], t1w[1][:].bitcast(U32), list1)
-        a_unit(0, 0)
-        a_unit(0, 1)
-        a_unit(0, 2)
-        a_unit(0, 3)
-        cast_weight("w1a0", 1, 0, sc)
-        cast_weight("w1a0", 1, 1, sc)
-        cast_weight("w1a1", 1, 0, sc)
-        cast_weight("w1a1", 1, 1, sc)
-        quantize_weight("w1a0", 1)
-        quantize_weight("w1a1", 1)
-        quantize_z(0, 0)
-        quantize_z(0, 1)
-        gather(v3w[:], t3w[:], list3)
-        cast_weight("w3", 0, 0, sc)
-        cast_weight("w3", 0, 1, sc)
-        a_unit(1, 0)
-        a_unit(1, 1)
-        a_unit(1, 2)
-        quantize_z(1, 0)
-        quantize_weight("w3", 0)
-        a_unit(1, 3)
-        deal(w4d[0][:], w4r[0][:], 4)
-        quantize_z(1, 1)
-        lim_unit(0, 0)
-        lim_unit(0, 1)
-        lim_unit(0, 2)
-        lim_unit(0, 3)
-        cast_weight("w3", 1, 0, sc)
-        cast_weight("w3", 1, 1, sc)
-        q_unit(0, 0, sc)
-        quantize_weight("w3", 1)
-        deal(w4d[1][:], w4r[1][:], 4)
-        lim_unit(1, 0)
-        lim_unit(1, 1)
-        lim_unit(1, 2)
-        lim_unit(1, 3)
-        q_unit(0, 1, sc)
-        planes(0, 0)
-        q_unit(1, 0, sc)
-        planes(0, 1)
-        q_unit(1, 1, vc, True)
-        planes(1, 0)
+        w1_0, w1_1 = w1[0:512, :], w1[512:1024, :]
+
+        cleared(nc.gpsimd, "t2s", 1024)
+        cleared(nc.gpsimd, "w2s", 2048)
+        cleared(nc.vector, "t1s", 2048)
+        cleared(nc.vector, "v2s1", 512)
+        cleared(nc.vector, "t3s", 2048)
+        cleared(nc.gpsimd, "w4s", 1024)
+        load_list("list2", offs2)
+        load_table("t2w0", tab2_words[0])
+        load_stacked("t2s", 0, tab2_scales)
+        load_weight("w1_00", w1_0, 0)
+        load_w2()
+        load_beside("w2s", 0, w2_scales)
+        load_table("t2w1", tab2_words[1])
+        load_weight("w1_10", w1_1, 0)
+        gather("v2w0", U32, sb["t2w0"][:].bitcast(U32), "list2")
+        gather("v2s0", U8, sb["t2s"][:], "list2")
+        nc.sync.dma_start(out=sb["v2s1"][0:100, :].bitcast(I32), in_=sb["v2s0"][4:104, :].bitcast(I32))
+        load_list("list1", offs)
+        load_table("t1w0", tab_words[0])
+        load_stacked("t1s", 4, tab_scales)
+        load_table("t1w1", tab_words[1])
+        load_list("list3", offs3)
+        load_beside("t3s", 0, tab3_scales)
+        load_t3w()
+        load_weight("w1_01", w1_0, 1)
+        load_weight("w1_11", w1_1, 1, 0, 256)
+        load_weight("w1_11b", w1_1, 1, 256, 512)
+        load_stacked("w4s", 8, w4_scales)
+        load_weight("w3_0", w3, 0, 0, 256)
+        load_weight("w3_0b", w3, 0, 256, 512)
+        load_w4(0)
+        load_weight("w3_1", w3, 1, 0, 256)
+        load_weight("w3_1b", w3, 1, 256, 512)
+        load_w4(1)
+
+        cast_weight("w1_00", sc)
+        deal("w2d", "w2r", 8)
+        deal("w2sd", "w2s", 16)
+        gather("v2w1", U32, sb["t2w1"][:].bitcast(U32), "list2", "w2r")
+        cast_weight("w1_10", sc)
+        quantize("w1_00", over="w2s")
+        for g in range(2):
+            for c in range(4):
+                b_pass(g, c, 0)
+                b_pass(g, c, 1)
+                park_b(g, c, "raw_w1_10")
+        gather("v1w0", U32, sb["t1w0"][:].bitcast(U32), "list1")
+        gather("v1s", U8, sb["t1s"][:], "list1")
+        quantize("w1_10")
+        for c in range(4):
+            a_pass(0, c, 0)
+        gather("v1w1", U32, sb["t1w1"][:].bitcast(U32), "list1")
+        gather("v3s", U8, sb["t3s"][:], "list3")
+        gather("v3w", U16, sb["t3w"][:], "list3")
+        cast_weight("w1_01", sc)
+        for c in range(4):
+            a_pass(0, c, 1)
+            product(0, c, "t3w")
+        cast_weight("w1_11", vc, 0, 64)
+        quantize("w1_01")
+        for c in range(4):
+            a_pass(1, c, 0)
+        cast_weight("w1_11", sc, 64, 128, "w1_11b", 64)
+        deal("w4sd", "w4s", 16)
+        quantize("w1_11")
+        quantize("z0", over="bf_w1_01")
+        cast_weight("w3_0", sc, 0, 64)
+        cast_weight("w3_0", sc, 64, 128, "w3_0b", 64)
+        for c in range(4):
+            a_pass(1, c, 1)
+        cast_weight("w3_1", sc, 0, 64)
+        deal("w4d0", "w4r0", 4)
+        product(1, 0, "w4r0")
+        product(1, 1)
+        quantize("w3_0")
+        quantize("z1", 0, 256)
+        lim_unit(0, 0, 0, "raw_w3_1")
+        lim_unit(0, 0, 1)
+        cast_weight("w3_1", sc, 64, 128, "w3_1b", 64)
+        lim_unit(0, 1, 0, "raw_w3_1b")
+        lim_unit(0, 1, 1)
+        product(1, 2)
+        product(1, 3)
+        quantize("z1", 256, 512)
+
+        spent = {(0, 0): "bf_w1_11", (0, 1): "raw_w1_01", (1, 0): "raw_w1_00", (1, 1): "raw_w3_0"}
+        for g in range(2):
+            for h in range(2):
+                for u in range(2):
+                    q_pass(g, h, u, 0)
+                    q_pass(g, h, u, 1)
+                    q_min(g, h, u, spent[(g, h)])
+                if (g, h) == (0, 0):
+                    quantize("w3_1")
+                    q_max(g, h)
+                    deal("w4d1", "w4r1", 4)
+                    for hh in range(2):
+                        for u in range(2):
+                            lim_unit(1, hh, u)
+                elif (g, h) == (1, 1):
+                    q_max(g, h, slice(0, 2))
+                    q_max(g, h, slice(2, 4))
+                    planes(1, 0)
+                else:
+                    planes(*divmod(2 * g + h - 1, 2))
+                    q_max(g, h)
+                round_y(g, h, vc if (g, h) == (1, 1) else sc)
         planes(1, 1)
-        for r in range(4):
-            nc.sync.dma_start(
-                out=out_2[:, r:16:4, :].rearrange("g q j -> q g j").bitcast(I32),
-                in_=y_scales[r:P:32, :, :].bitcast(I32),
-            )
+        store_scales()

@@ -78,14 +78,23 @@ def tile_list_stamp_trade_limits_kernel(
                     in_=scales[:, r:16:4, :].rearrange("a q n -> q a n").bitcast(I32),
                 )
 
+        def load_rows(name, row0, scales):
+            for a in range(scales.shape[0]):
+                for r in range(4):
+                    nc.sync.dma_start(
+                        out=sb[name][row0 + 4 * a + r : P : 32, :].bitcast(I32), in_=scales[a, r:16:4, :].bitcast(I32)
+                    )
+
         def load_weight(name, rows, g, c0=0, c1=G):
             nc.sync.dma_start(
                 out=held("raw_" + name, [P, 4, c1 - c0], F32)[:],
                 in_=rows.rearrange("(p i) c -> p i c", i=4)[:, :, G * g + c0 : G * g + c1],
             )
 
-        def gather(name, dtype, window, lst, over=None):
-            nc.vector.tensor_copy(out=held(name, [P, S], dtype, over)[:], in_=window.indirect(sb[lst][:]))
+        def gather(name, dtype, window, lst, over=None, j0=0, j1=S):
+            if j0 == 0:
+                held(name, [P, S], dtype, over)
+            nc.vector.tensor_copy(out=sb[name][:, j0:j1], in_=window.indirect(sb[lst][:, j0 // 16 : j1 // 16]))
 
         def deal(name, src, run, over=None):
             dst = held(name, list(sb[src].shape), sb[src].dtype, over)
@@ -116,23 +125,19 @@ def tile_list_stamp_trade_limits_kernel(
         def opened(key, index, shape):
             banks[key] = psum.tile(shape, F32, name="bank%d" % index)
 
-        def b_pass(g, c, a):
-            if a == 0:
-                opened(("b", g, c), 4 * g + c, [P, 4, P])
-            js = slice(P * c, P * c + P)
-            for t in range(4):
+        def b_unit(g, t, over=None):
+            opened(("b", g, t), 4 * g + t, [P, S])
+            for a in range(2):
                 cols = slice(1024 * a + G * g + P * t, 1024 * a + G * g + P * t + P)
                 nc.tensor.matmul_mx(
-                    out=banks[("b", g, c)][:, t, :],
+                    out=banks[("b", g, t)][:],
                     lhsT=sb["w2d"][:, cols].bitcast(FP4X4), lhsT_scale=sb["w2sd"][:, cols],
-                    rhs=sb["v2w%d" % a][:, js].bitcast(FP8X4), rhs_scale=sb["v2s%d" % a][:, js],
-                    start=(a == 0 and t == 0), stop=(a == 1 and t == 3),
+                    rhs=sb["v2w%d" % a][:].bitcast(FP8X4), rhs_scale=sb["v2s%d" % a][:],
+                    start=(a == 0), stop=(a == 1),
                 )
-
-        def park_b(g, c, over=None):
-            if g == 0 and c == 0:
-                held("b", [P, 2, 4, 64, 4, 2], F32, over)
-            nc.scalar.copy(out=sb["b"][:, g, c], in_=banks[("b", g, c)][:].rearrange("p t (j e) -> p j t e", e=2))
+            if g == 0 and t == 0:
+                held("b", [P, 2, 4, S], F32, over)
+            nc.scalar.copy(out=sb["b"][:, g, t, :], in_=banks[("b", g, t)][:])
 
         def a_pass(g, c, a):
             if a == 0:
@@ -153,7 +158,8 @@ def tile_list_stamp_trade_limits_kernel(
                 held("bf_z%d" % g, [P, 2048], BF16, over)
             nc.vector.tensor_tensor(
                 out=sb["bf_z%d" % g][:, G * c : G * c + G].rearrange("p (j e t) -> p j t e", e=2, t=4),
-                in0=banks[("a", g, c)][:].rearrange("p t (j e) -> p j t e", e=2), in1=sb["b"][:, g, c], op=ALU.mult,
+                in0=banks[("a", g, c)][:].rearrange("p t (j e) -> p j t e", e=2), in1=sb["b"][:, g, :, P * c : P * c + P].rearrange("p t (j e) -> p j t e", e=2),
+                op=ALU.mult,
             )
 
         def lim_unit(g, h, u, over=None):
@@ -232,33 +238,32 @@ def tile_list_stamp_trade_limits_kernel(
         vc = nc.vector.tensor_copy
         w1_0, w1_1 = w1[0:512, :], w1[512:1024, :]
 
-        cleared(nc.gpsimd, "t2s", 1024)
+        cleared(nc.gpsimd, "t2s", 2048)
         cleared(nc.gpsimd, "w2s", 2048)
         cleared(nc.vector, "t1s", 2048)
-        cleared(nc.vector, "v2s1", 512)
         cleared(nc.vector, "t3s", 2048)
         cleared(nc.gpsimd, "w4s", 1024)
         load_list("list2", offs2)
         load_table("t2w0", tab2_words[0])
-        load_stacked("t2s", 0, tab2_scales)
+        load_beside("t2s", 0, tab2_scales)
         load_weight("w1_00", w1_0, 0)
         load_w2()
         load_beside("w2s", 0, w2_scales)
         load_table("t2w1", tab2_words[1])
-        load_weight("w1_10", w1_1, 0)
+        load_list("list3", offs3)
         gather("v2w0", U32, sb["t2w0"][:].bitcast(U32), "list2")
-        gather("v2s0", U8, sb["t2s"][:], "list2")
-        nc.sync.dma_start(out=sb["v2s1"][0:100, :].bitcast(I32), in_=sb["v2s0"][4:104, :].bitcast(I32))
-        load_list("list1", offs)
+        gather("v2s0", U8, sb["t2s"][:, 0:1024], "list2")
+        gather("v2s1", U8, sb["t2s"][:, 1024:2048], "list2")
+        load_weight("w1_10", w1_1, 0)
+        load_beside("t3s", 0, tab3_scales)
         load_table("t1w0", tab_words[0])
+        load_list("list1", offs)
         load_stacked("t1s", 4, tab_scales)
         load_table("t1w1", tab_words[1])
-        load_list("list3", offs3)
-        load_beside("t3s", 0, tab3_scales)
-        load_t3w()
         load_weight("w1_01", w1_0, 1)
         load_weight("w1_11", w1_1, 1, 0, 256)
         load_weight("w1_11b", w1_1, 1, 256, 512)
+        load_t3w()
         load_stacked("w4s", 8, w4_scales)
         load_weight("w3_0", w3, 0, 0, 256)
         load_weight("w3_0b", w3, 0, 256, 512)
@@ -274,29 +279,28 @@ def tile_list_stamp_trade_limits_kernel(
         cast_weight("w1_10", sc)
         quantize("w1_00", over="w2s")
         for g in range(2):
-            for c in range(4):
-                b_pass(g, c, 0)
-                b_pass(g, c, 1)
-                park_b(g, c, "raw_w1_10")
+            for t in range(4):
+                b_unit(g, t, "raw_w1_10")
+        gather("v3s", U8, sb["t3s"][:], "list3")
         gather("v1w0", U32, sb["t1w0"][:].bitcast(U32), "list1")
         gather("v1s", U8, sb["t1s"][:], "list1")
-        quantize("w1_10")
+        quantize("w1_10", over="t1w0")
         for c in range(4):
             a_pass(0, c, 0)
-        gather("v1w1", U32, sb["t1w1"][:].bitcast(U32), "list1")
-        gather("v3s", U8, sb["t3s"][:], "list3")
-        gather("v3w", U16, sb["t3w"][:], "list3")
+        gather("v1w1", U32, sb["t1w1"][:].bitcast(U32), "list1", None, 0, 256)
+        gather("v1w1", U32, sb["t1w1"][:].bitcast(U32), "list1", None, 256, 512)
         cast_weight("w1_01", sc)
         for c in range(4):
             a_pass(0, c, 1)
-            product(0, c, "t3w")
+            product(0, c)
         cast_weight("w1_11", vc, 0, 64)
         quantize("w1_01")
         for c in range(4):
             a_pass(1, c, 0)
         cast_weight("w1_11", sc, 64, 128, "w1_11b", 64)
-        deal("w4sd", "w4s", 16)
+        gather("v3w", U16, sb["t3w"][:], "list3", "raw_w1_11")
         quantize("w1_11")
+        deal("w4sd", "w4s", 16)
         quantize("z0", over="bf_w1_01")
         cast_weight("w3_0", sc, 0, 64)
         cast_weight("w3_0", sc, 64, 128, "w3_0b", 64)

@@ -242,7 +242,9 @@ def tile_list_stamp_trade_limits_kernel(
         cleared(nc.gpsimd, "w2s", 2048)
         cleared(nc.vector, "t1s", 2048)
         cleared(nc.vector, "t3s", 2048)
-        cleared(nc.gpsimd, "w4s", 1024)
+        cleared(nc.vector, "w4s", 1024)
+        load_stacked("t1s", 4, tab_scales, nc.gpsimd)
+        load_stacked("w4s", 8, w4_scales, nc.gpsimd)
         load_list("list2", offs2)
         load_table("t2w0", tab2_words[0])
         load_beside("t2s", 0, tab2_scales)
@@ -250,21 +252,19 @@ def tile_list_stamp_trade_limits_kernel(
         load_w2()
         load_beside("w2s", 0, w2_scales)
         load_table("t2w1", tab2_words[1])
-        load_list("list3", offs3)
+        load_list("list1", offs)
         gather("v2w0", U32, sb["t2w0"][:].bitcast(U32), "list2")
         gather("v2s0", U8, sb["t2s"][:, 0:1024], "list2")
         gather("v2s1", U8, sb["t2s"][:, 1024:2048], "list2")
         load_weight("w1_10", w1_1, 0)
-        load_beside("t3s", 0, tab3_scales)
         load_table("t1w0", tab_words[0])
-        load_list("list1", offs)
-        load_stacked("t1s", 4, tab_scales)
+        load_list("list3", offs3)
+        load_beside("t3s", 0, tab3_scales)
         load_table("t1w1", tab_words[1])
         load_weight("w1_01", w1_0, 1)
         load_weight("w1_11", w1_1, 1, 0, 256)
         load_weight("w1_11b", w1_1, 1, 256, 512)
         load_t3w()
-        load_stacked("w4s", 8, w4_scales)
         load_weight("w3_0", w3, 0, 0, 256)
         load_weight("w3_0b", w3, 0, 256, 512)
         load_w4(0)
@@ -281,9 +281,9 @@ def tile_list_stamp_trade_limits_kernel(
         for g in range(2):
             for t in range(4):
                 b_unit(g, t, "raw_w1_10")
-        gather("v3s", U8, sb["t3s"][:], "list3")
-        gather("v1w0", U32, sb["t1w0"][:].bitcast(U32), "list1")
         gather("v1s", U8, sb["t1s"][:], "list1")
+        gather("v1w0", U32, sb["t1w0"][:].bitcast(U32), "list1")
+        gather("v3s", U8, sb["t3s"][:], "list3")
         quantize("w1_10", over="t1w0")
         for c in range(4):
             a_pass(0, c, 0)
@@ -300,7 +300,7 @@ def tile_list_stamp_trade_limits_kernel(
         cast_weight("w1_11", sc, 64, 128, "w1_11b", 64)
         gather("v3w", U16, sb["t3w"][:], "list3", "raw_w1_11")
         quantize("w1_11")
-        deal("w4sd", "w4s", 16)
+        deal("w4sd", "w4s", 16, "t3w")
         quantize("z0", over="bf_w1_01")
         cast_weight("w3_0", sc, 0, 64)
         cast_weight("w3_0", sc, 64, 128, "w3_0b", 64)

@@ -107,8 +107,8 @@ def tile_list_stamp_trade_limits_kernel(
             if "bf_" + name not in sb:
                 held("bf_" + name, [P, 2048], BF16, over)
             copy(
-                out=sb["bf_" + name][:].rearrange("p (t m i) -> p m i t", t=4, i=4)[:, m0:m1],
-                in_=sb["raw_" + (src or name)][:].rearrange("p i (m t) -> p m i t", t=4)[:, m0 - base : m1 - base],
+                out=sb["bf_" + name][:].rearrange("p (t m u e) -> p m u t e", t=4, u=2, e=2)[:, m0:m1],
+                in_=sb["raw_" + (src or name)][:].rearrange("p (u e) (m t) -> p m u t e", t=4, e=2)[:, m0 - base : m1 - base],
             )
 
         def quantize(name, c0=0, c1=G, over=None):
@@ -215,8 +215,8 @@ def tile_list_stamp_trade_limits_kernel(
 
         def round_y(g, h, copy, over=None):
             copy(
-                out=held("bf_y%d%d" % (g, h), [P, 256, 4], BF16, over)[:].rearrange("p (c i) t -> p c t i", i=4),
-                in_=sb["y%d%d" % (g, h)][:].rearrange("p t (c i) -> p c t i", i=4),
+                out=held("bf_y%d%d" % (g, h), [P, 256, 4], BF16, over)[:].rearrange("p (c i) (u e) -> p c u i e", i=4, e=2),
+                in_=sb["y%d%d" % (g, h)][:].rearrange("p (u e) (c i) -> p c u i e", i=4, e=2),
             )
 
         def planes(g, h):

@@ -293,7 +293,7 @@ def tile_list_stamp_trade_limits_kernel(
         for c in range(4):
             a_pass(0, c, 1)
             product(0, c)
-        cast_weight("w1_11", vc, 0, 64)
+        cast_weight("w1_11", sc, 0, 64)
         quantize("w1_01")
         for c in range(4):
             a_pass(1, c, 0)

@@ -31,8 +31,11 @@ def tile_list_stamp_trade_limits_kernel(
 
         sb = {}
 
+        tags = {}
+
         def held(name, shape, dtype, over=None):
-            sb[name] = keep.tile(shape, dtype, name=name, tag=over or name, align_bytes=64)
+            tags[name] = tags[over] if over else name
+            sb[name] = keep.tile(shape, dtype, name=name, tag=tags[name], align_bytes=64)
             return sb[name]
 
         def words4(src):
@@ -213,19 +216,20 @@ def tile_list_stamp_trade_limits_kernel(
             )
             nc.sync.dma_start(out=out_rows[g][:, ts, 256 * h : 256 * h + 256], in_=sb["y%d%d" % (g, h)][:, ts, :])
 
-        def round_y(g, h, copy, over=None):
+        def round_y(g, h, copy, j0=0, j1=256):
+            if "bf_y%d" % g not in sb:
+                held("bf_y%d" % g, [P, S, 4], BF16)
             copy(
-                out=held("bf_y%d%d" % (g, h), [P, 256, 4], BF16, over)[:].rearrange("p (c i) (u e) -> p c u i e", i=4, e=2),
-                in_=sb["y%d%d" % (g, h)][:].rearrange("p (u e) (c i) -> p c u i e", i=4, e=2),
+                out=sb["bf_y%d" % g][:, 256 * h + j0 : 256 * h + j1].rearrange("p (c i) (u e) -> p c u i e", i=4, e=2),
+                in_=sb["y%d%d" % (g, h)][:, :, j0:j1].rearrange("p (u e) (c i) -> p c u i e", i=4, e=2),
             )
 
-        def planes(g, h):
-            js = slice(256 * h, 256 * h + 256)
+        def planes(g, j0, j1):
             nc.vector.quantize_mx(
-                out=y_codes[:, g, js].bitcast(FP8X4), scales=y_scales[:, g, js],
-                in_=sb["bf_y%d%d" % (g, h)][:].rearrange("p j t -> p (j t)"),
+                out=y_codes[:, g, j0:j1].bitcast(FP8X4), scales=y_scales[:, g, j0:j1],
+                in_=sb["bf_y%d" % g][:, j0:j1].rearrange("p j t -> p (j t)"),
             )
-            nc.sync.dma_start(out=words4(out_1[g])[:, js], in_=y_codes[:, g, js])
+            nc.sync.dma_start(out=words4(out_1[g])[:, j0:j1], in_=y_codes[:, g, j0:j1])
 
         def store_scales():
             for r in range(4):
@@ -262,8 +266,7 @@ def tile_list_stamp_trade_limits_kernel(
         load_beside("t3s", 0, tab3_scales)
         load_table("t1w1", tab_words[1])
         load_weight("w1_01", w1_0, 1)
-        load_weight("w1_11", w1_1, 1, 0, 256)
-        load_weight("w1_11b", w1_1, 1, 256, 512)
+        load_weight("w1_11", w1_1, 1)
         load_t3w()
         load_weight("w3_0", w3, 0, 0, 256)
         load_weight("w3_0b", w3, 0, 256, 512)
@@ -284,7 +287,7 @@ def tile_list_stamp_trade_limits_kernel(
         gather("v1s", U8, sb["t1s"][:], "list1")
         gather("v1w0", U32, sb["t1w0"][:].bitcast(U32), "list1")
         gather("v3s", U8, sb["t3s"][:], "list3")
-        quantize("w1_10", over="t1w0")
+        quantize("w1_10", over="t1s")
         for c in range(4):
             a_pass(0, c, 0)
         gather("v1w1", U32, sb["t1w1"][:].bitcast(U32), "list1", None, 0, 256)
@@ -293,15 +296,14 @@ def tile_list_stamp_trade_limits_kernel(
         for c in range(4):
             a_pass(0, c, 1)
             product(0, c)
-        cast_weight("w1_11", sc, 0, 64)
+        cast_weight("w1_11", sc)
         quantize("w1_01")
         for c in range(4):
             a_pass(1, c, 0)
-        cast_weight("w1_11", sc, 64, 128, "w1_11b", 64)
         gather("v3w", U16, sb["t3w"][:], "list3", "raw_w1_11")
         quantize("w1_11")
-        deal("w4sd", "w4s", 16, "t3w")
-        quantize("z0", over="bf_w1_01")
+        deal("w4sd", "w4s", 16, "bf_z0")
+        quantize("z0", over="raw_w1_01")
         cast_weight("w3_0", sc, 0, 64)
         cast_weight("w3_0", sc, 64, 128, "w3_0b", 64)
         for c in range(4):
@@ -321,27 +323,37 @@ def tile_list_stamp_trade_limits_kernel(
         product(1, 3)
         quantize("z1", 256, 512)
 
-        spent = {(0, 0): "bf_w1_11", (0, 1): "raw_w1_01", (1, 0): "raw_w1_00", (1, 1): "raw_w3_0"}
-        for g in range(2):
-            for h in range(2):
-                for u in range(2):
-                    q_pass(g, h, u, 0)
-                    q_pass(g, h, u, 1)
-                    q_min(g, h, u, spent[(g, h)])
-                if (g, h) == (0, 0):
-                    quantize("w3_1")
-                    q_max(g, h)
-                    deal("w4d1", "w4r1", 4)
-                    for hh in range(2):
-                        for u in range(2):
-                            lim_unit(1, hh, u)
-                elif (g, h) == (1, 1):
-                    q_max(g, h, slice(0, 2))
-                    q_max(g, h, slice(2, 4))
-                    planes(1, 0)
-                else:
-                    planes(*divmod(2 * g + h - 1, 2))
-                    q_max(g, h)
-                round_y(g, h, vc if (g, h) == (1, 1) else sc)
-        planes(1, 1)
+        for u in range(2):
+            q_pass(0, 0, u, 0)
+            q_pass(0, 0, u, 1)
+            q_min(0, 0, u, "bf_w1_11")
+        quantize("w3_1")
+        q_max(0, 0)
+        deal("w4d1", "w4r1", 4)
+        for hh in range(2):
+            for u in range(2):
+                lim_unit(1, hh, u)
+        round_y(0, 0, sc)
+        for u in range(2):
+            q_pass(0, 1, u, 0)
+            q_pass(0, 1, u, 1)
+            q_min(0, 1, u, "t1w1")
+        q_max(0, 1)
+        round_y(0, 1, sc)
+        for u in range(2):
+            q_pass(1, 0, u, 0)
+            q_pass(1, 0, u, 1)
+            q_min(1, 0, u, "raw_w1_00")
+        q_max(1, 0)
+        round_y(1, 0, sc)
+        for u in range(2):
+            q_pass(1, 1, u, 0)
+            q_pass(1, 1, u, 1)
+            q_min(1, 1, u, "raw_w3_0")
+        planes(0, 0, S)
+        q_max(1, 1)
+        round_y(1, 1, sc, 0, 128)
+        planes(1, 0, 256)
+        round_y(1, 1, vc, 128, 256)
+        planes(1, 256, S)
         store_scales()

@@ -344,16 +344,17 @@ def tile_list_stamp_trade_limits_kernel(
             q_pass(1, 0, u, 0)
             q_pass(1, 0, u, 1)
             q_min(1, 0, u, "raw_w1_00")
+        planes(0, 0, 256)
         q_max(1, 0)
         round_y(1, 0, sc)
         for u in range(2):
             q_pass(1, 1, u, 0)
             q_pass(1, 1, u, 1)
             q_min(1, 1, u, "raw_w3_0")
-        planes(0, 0, S)
-        q_max(1, 1)
-        round_y(1, 1, sc, 0, 128)
+        planes(0, 256, S)
+        q_max(1, 1, slice(0, 2))
+        q_max(1, 1, slice(2, 4))
         planes(1, 0, 256)
-        round_y(1, 1, vc, 128, 256)
+        round_y(1, 1, vc)
         planes(1, 256, S)
         store_scales()

@@ -269,8 +269,8 @@ def tile_list_stamp_trade_limits_kernel(
         load_weight("w1_11", w1_1, 1)
         load_t3w()
         load_weight("w3_0", w3, 0, 0, 256)
-        load_weight("w3_0b", w3, 0, 256, 512)
         load_w4(0)
+        load_weight("w3_0b", w3, 0, 256, 512)
         load_weight("w3_1", w3, 1, 0, 256)
         load_weight("w3_1b", w3, 1, 256, 512)
         load_w4(1)
@@ -300,7 +300,7 @@ def tile_list_stamp_trade_limits_kernel(
         quantize("w1_01")
         for c in range(4):
             a_pass(1, c, 0)
-        gather("v3w", U16, sb["t3w"][:], "list3", "raw_w1_11")
+        gather("v3w", U16, sb["t3w"][:], "list3")
         quantize("w1_11")
         deal("w4sd", "w4s", 16, "bf_z0")
         quantize("z0", over="raw_w1_01")

@@ -99,11 +99,12 @@ def tile_list_stamp_trade_limits_kernel(
                 held(name, [P, S], dtype, over)
             nc.vector.tensor_copy(out=sb[name][:, j0:j1], in_=window.indirect(sb[lst][:, j0 // 16 : j1 // 16]))
 
-        def deal(name, src, run, over=None):
+        def deal(name, src, run, over=None, copy=nc.vector.tensor_copy, dtype=None):
             dst = held(name, list(sb[src].shape), sb[src].dtype, over)
-            nc.vector.tensor_copy(
-                out=dst[:].rearrange("p (g t b m) -> p g b t m", t=4, m=run, b=P // run),
-                in_=sb[src][:].rearrange("p (g b m t) -> p g b t m", t=4, m=run, b=P // run),
+            dtype = dtype or sb[src].dtype
+            copy(
+                out=dst[:].bitcast(dtype).rearrange("p (g t b m) -> p g b t m", t=4, m=run, b=P // run),
+                in_=sb[src][:].bitcast(dtype).rearrange("p (g b m t) -> p g b t m", t=4, m=run, b=P // run),
             )
 
         def cast_weight(name, copy, m0=0, m1=P, src=None, base=0, over=None):
@@ -166,7 +167,7 @@ def tile_list_stamp_trade_limits_kernel(
             )
 
         def lim_unit(g, h, u, over=None):
-            opened(("lim", g, h, u), 2 * h + u, [P, 2, 256])
+            opened(("lim", g, h, u), 4 * h + u, [P, 2, 256])
             bank = banks[("lim", g, h, u)]
             js = slice(256 * h, 256 * h + 256)
             for e in range(2):
@@ -182,7 +183,7 @@ def tile_list_stamp_trade_limits_kernel(
 
         def q_pass(g, h, u, a):
             if a == 0:
-                opened(("q", g, h, u), 4 + 2 * h + u, [P, 2, 256])
+                opened(("q", g, h, u), 2 + 4 * h + u, [P, 2, 256])
             js = slice(256 * h, 256 * h + 256)
             for e in range(2):
                 t = 2 * u + e
@@ -310,6 +311,8 @@ def tile_list_stamp_trade_limits_kernel(
             a_pass(1, c, 1)
         cast_weight("w3_1", sc, 0, 64)
         deal("w4d0", "w4r0", 4)
+        for u in range(2):
+            q_pass(0, 0, u, 0)
         product(1, 0, "w4r0")
         product(1, 1)
         quantize("w3_0")
@@ -319,20 +322,19 @@ def tile_list_stamp_trade_limits_kernel(
         cast_weight("w3_1", sc, 64, 128, "w3_1b", 64)
         lim_unit(0, 1, 0, "raw_w3_1b")
         lim_unit(0, 1, 1)
+        deal("w4d1", "w4r1", 4, "c_w3_0", sc, U32)
         product(1, 2)
         product(1, 3)
         quantize("z1", 256, 512)
 
         for u in range(2):
-            q_pass(0, 0, u, 0)
             q_pass(0, 0, u, 1)
             q_min(0, 0, u, "bf_w1_11")
         quantize("w3_1")
         q_max(0, 0)
-        deal("w4d1", "w4r1", 4)
         for hh in range(2):
             for u in range(2):
-                lim_unit(1, hh, u)
+                lim_unit(1, hh, u, "w4r1" if hh == 0 else None)
         round_y(0, 0, sc)
         for u in range(2):
             q_pass(0, 1, u, 0)

from contextlib import ExitStack

import concourse.mybir as mybir

FLOPS = 3758096384

F32 = mybir.dt.float32
BF16 = mybir.dt.bfloat16
I32 = mybir.dt.int32
U32 = mybir.dt.uint32
U16 = mybir.dt.uint16
U8 = mybir.dt.uint8
FP8X4 = mybir.dt.float8_e4m3fn_x4
FP4X4 = mybir.dt.float4_e2m1fn_x4
ALU = mybir.AluOpType
ACT = mybir.ActivationFunctionType

P = 128
S = 512
G = 512


def tile_list_stamp_trade_limits_kernel(
    tc, tab_words, tab_scales, tab2_words, tab2_scales, tab3_words, tab3_scales, offs, offs2, offs3,
    w1, w2_words, w2_scales, w3, w4_words, w4_scales, out_0, out_1, out_2,
):
    nc = tc.nc
    with ExitStack() as ctx:
        keep = ctx.enter_context(tc.tile_pool(name="keep", bufs=1))
        psum = ctx.enter_context(tc.psum_pool(name="psum", bufs=1))

        sb = {}

        tags = {}

        def held(name, shape, dtype, over=None):
            tags[name] = tags[over] if over else name
            sb[name] = keep.tile(shape, dtype, name=name, tag=tags[name], align_bytes=64)
            return sb[name]

        def words4(src):
            return src.rearrange("p n i -> p (n i)").bitcast(I32)

        def load_list(name, src):
            nc.sync.dma_start(held(name, [P, 32], U16)[:], src)

        def load_table(name, src):
            nc.sync.dma_start(out=held(name, [P, src.shape[1]], I32)[:], in_=words4(src))

        def load_t3w():
            nc.sync.dma_start(out=held("t3w", [P, 2048], U16)[:].bitcast(I32), in_=tab3_words[0].bitcast(I32))

        def load_w2():
            nc.sync.dma_start(
                out=held("w2r", [P, 2048], U16)[:].bitcast(I32).rearrange("p (a n) -> p a n", a=2),
                in_=w2_words.rearrange("a p n -> p a n").bitcast(I32),
            )

        def load_w4(g):
            nc.sync.dma_start(
                out=held("w4r%d" % g, [P, 1024], I32)[:].rearrange("p (a n) -> p a n", a=2),
                in_=w4_words.rearrange("a p n i -> p a (n i)").bitcast(I32)[:, :, G * g : G * g + G],
            )

        def cleared(engine, name, width):
            engine.memset(held(name, [P, width], U8)[:].bitcast(I32), 0)

        def load_stacked(name, row0, scales, queue=nc.sync):
            n = scales.shape[0]
            for q in range(4):
                queue.dma_start(
                    out=sb[name][32 * q + row0 : 32 * q + row0 + 4 * n, :].bitcast(I32),
                    in_=scales[:, 4 * q : 4 * q + 4, :].bitcast(I32),
                )

        def load_beside(name, row0, scales, queue=nc.sync):
            n = scales.shape[0]
            for r in range(4):
                queue.dma_start(
                    out=sb[name][row0 + r : P : 32, :].bitcast(I32).rearrange("q (a n) -> q a n", a=n),
                    in_=scales[:, r:16:4, :].rearrange("a q n -> q a n").bitcast(I32),
                )

        def load_rows(name, row0, scales):
            for a in range(scales.shape[0]):
                for r in range(4):
                    nc.sync.dma_start(
                        out=sb[name][row0 + 4 * a + r : P : 32, :].bitcast(I32), in_=scales[a, r:16:4, :].bitcast(I32)
                    )

        def load_weight(name, rows, g, c0=0, c1=G):
            nc.sync.dma_start(
                out=held("raw_" + name, [P, 4, c1 - c0], F32)[:],
                in_=rows.rearrange("(p i) c -> p i c", i=4)[:, :, G * g + c0 : G * g + c1],
            )

        def gather(name, dtype, window, lst, over=None, j0=0, j1=S):
            if j0 == 0:
                held(name, [P, S], dtype, over)
            nc.vector.tensor_copy(out=sb[name][:, j0:j1], in_=window.indirect(sb[lst][:, j0 // 16 : j1 // 16]))

        def deal(name, src, run, over=None, copy=nc.vector.tensor_copy, dtype=None):
            dst = held(name, list(sb[src].shape), sb[src].dtype, over)
            dtype = dtype or sb[src].dtype
            copy(
                out=dst[:].bitcast(dtype).rearrange("p (g t b m) -> p g b t m", t=4, m=run, b=P // run),
                in_=sb[src][:].bitcast(dtype).rearrange("p (g b m t) -> p g b t m", t=4, m=run, b=P // run),
            )

        def cast_weight(name, copy, m0=0, m1=P, src=None, base=0, over=None):
            if "bf_" + name not in sb:
                held("bf_" + name, [P, 2048], BF16, over)
            copy(
                out=sb["bf_" + name][:].rearrange("p (t m u e) -> p m u t e", t=4, u=2, e=2)[:, m0:m1],
                in_=sb["raw_" + (src or name)][:].rearrange("p (u e) (m t) -> p m u t e", t=4, e=2)[:, m0 - base : m1 - base],
            )

        def quantize(name, c0=0, c1=G, over=None):
            if c0 == 0:
                held("c_" + name, [P, G], U32, over)
                held("s_" + name, [P, G], U8)
            nc.vector.quantize_mx(
                out=sb["c_" + name][:, c0:c1].bitcast(FP8X4), scales=sb["s_" + name][:, c0:c1],
                in_=sb["bf_" + name][:, 4 * c0 : 4 * c1],
            )

        banks = {}

        def opened(key, index, shape):
            banks[key] = psum.tile(shape, F32, name="bank%d" % index)

        def b_unit(g, t, over=None):
            opened(("b", g, t), 4 * g + t, [P, S])
            for a in range(2):
                cols = slice(1024 * a + G * g + P * t, 1024 * a + G * g + P * t + P)
                nc.tensor.matmul_mx(
                    out=banks[("b", g, t)][:],
                    lhsT=sb["w2d"][:, cols].bitcast(FP4X4), lhsT_scale=sb["w2sd"][:, cols],
                    rhs=sb["v2w%d" % a][:].bitcast(FP8X4), rhs_scale=sb["v2s%d" % a][:],
                    start=(a == 0), stop=(a == 1),
                )
            if g == 0 and t == 0:
                held("b", [P, 2, 4, S], F32, over)
            nc.scalar.copy(out=sb["b"][:, g, t, :], in_=banks[("b", g, t)][:])

        def a_pass(g, c, a):
            if a == 0:
                opened(("a", g, c), 4 * g + c, [P, 4, P])
            js = slice(P * c, P * c + P)
            for t in range(4):
                cols = slice(P * t, P * t + P)
                nc.tensor.matmul_mx(
                    out=banks[("a", g, c)][:, t, :],
                    lhsT=sb["c_w1_%d%d" % (a, g)][:, cols].bitcast(FP8X4),
                    lhsT_scale=sb["s_w1_%d%d" % (a, g)][:, cols],
                    rhs=sb["v1w%d" % a][:, js].bitcast(FP8X4), rhs_scale=sb["v1s"][4 + 4 * a :, js],
                    start=(a == 0 and t == 0), stop=(a == 1 and t == 3),
                )

        def product(g, c, over=None):
            if c == 0:
                held("bf_z%d" % g, [P, 2048], BF16, over)
            nc.vector.tensor_tensor(
                out=sb["bf_z%d" % g][:, G * c : G * c + G].rearrange("p (j e t) -> p j t e", e=2, t=4),
                in0=banks[("a", g, c)][:].rearrange("p t (j e) -> p j t e", e=2), in1=sb["b"][:, g, :, P * c : P * c + P].rearrange("p t (j e) -> p j t e", e=2),
                op=ALU.mult,
            )

        def lim_unit(g, h, u, over=None):
            opened(("lim", g, h, u), 4 * h + u, [P, 2, 256])
            bank = banks[("lim", g, h, u)]
            js = slice(256 * h, 256 * h + 256)
            for e in range(2):
                cols = slice(P * (2 * u + e), P * (2 * u + e) + P)
                nc.tensor.matmul_mx(
                    out=bank[:, e, :],
                    lhsT=sb["c_w3_%d" % g][:, cols].bitcast(FP8X4), lhsT_scale=sb["s_w3_%d" % g][:, cols],
                    rhs=sb["v3w"][:, js].bitcast(FP4X4), rhs_scale=sb["v3s"][:, js], start=True, stop=True,
                )
            if u == 0:
                held("lim%d%d" % (g, h), [P, 4, 256], F32, over)
            nc.scalar.activation(out=sb["lim%d%d" % (g, h)][:, 2 * u : 2 * u + 2, :], in_=bank[:], func=ACT.Abs)

        def q_pass(g, h, u, a):
            if a == 0:
                opened(("q", g, h, u), 2 + 4 * h + u, [P, 2, 256])
            js = slice(256 * h, 256 * h + 256)
            for e in range(2):
                t = 2 * u + e
                nc.tensor.matmul_mx(
                    out=banks[("q", g, h, u)][:, e, :],
                    lhsT=sb["w4d%d" % g][:, G * a + P * t : G * a + P * t + P].bitcast(FP8X4),
                    lhsT_scale=sb["w4sd"][8 + 4 * a :, G * g + P * t : G * g + P * t + P],
                    rhs=sb["c_z%d" % a][:, js].bitcast(FP8X4), rhs_scale=sb["s_z%d" % a][:, js],
                    start=(a == 0 and e == 0), stop=(a == 1 and e == 1),
                )

        y_codes = held("y_codes", [P, 2, S], I32)
        y_scales = held("y_scales", [P, 2, S], U8)
        out_rows = out_0.rearrange("(g p t) j -> g p t j", t=4, p=P)

        def q_min(g, h, u, over=None):
            if u == 0:
                held("low%d%d" % (g, h), [P, 4, 256], F32, over)
            ts = slice(2 * u, 2 * u + 2)
            nc.vector.tensor_tensor(
                out=sb["low%d%d" % (g, h)][:, ts, :], in0=banks[("q", g, h, u)][:], in1=sb["lim%d%d" % (g, h)][:, ts, :],
                op=ALU.min,
            )

        def q_max(g, h, ts=slice(0, 4), over=None):
            if ts.start == 0:
                held("y%d%d" % (g, h), [P, 4, 256], F32, over)
            nc.vector.scalar_tensor_tensor(
                out=sb["y%d%d" % (g, h)][:, ts, :], in0=sb["lim%d%d" % (g, h)][:, ts, :], scalar=-1.0,
                in1=sb["low%d%d" % (g, h)][:, ts, :], op0=ALU.mult, op1=ALU.max,
            )
            nc.sync.dma_start(out=out_rows[g][:, ts, 256 * h : 256 * h + 256], in_=sb["y%d%d" % (g, h)][:, ts, :])

        def round_y(g, h, copy, j0=0, j1=256):
            if "bf_y%d" % g not in sb:
                held("bf_y%d" % g, [P, S, 4], BF16)
            copy(
                out=sb["bf_y%d" % g][:, 256 * h + j0 : 256 * h + j1].rearrange("p (c i) (u e) -> p c u i e", i=4, e=2),
                in_=sb["y%d%d" % (g, h)][:, :, j0:j1].rearrange("p (u e) (c i) -> p c u i e", i=4, e=2),
            )

        def planes(g, j0, j1):
            nc.vector.quantize_mx(
                out=y_codes[:, g, j0:j1].bitcast(FP8X4), scales=y_scales[:, g, j0:j1],
                in_=sb["bf_y%d" % g][:, j0:j1].rearrange("p j t -> p (j t)"),
            )
            nc.sync.dma_start(out=words4(out_1[g])[:, j0:j1], in_=y_codes[:, g, j0:j1])

        def store_scales():
            for r in range(4):
                nc.sync.dma_start(
                    out=out_2[:, r:16:4, :].rearrange("g q j -> q g j").bitcast(I32),
                    in_=y_scales[r:P:32, :, :].bitcast(I32),
                )

        sc = nc.scalar.copy
        vc = nc.vector.tensor_copy
        w1_0, w1_1 = w1[0:512, :], w1[512:1024, :]

        cleared(nc.gpsimd, "t2s", 2048)
        cleared(nc.gpsimd, "w2s", 2048)
        cleared(nc.vector, "t1s", 2048)
        cleared(nc.vector, "t3s", 2048)
        cleared(nc.vector, "w4s", 1024)
        load_stacked("t1s", 4, tab_scales, nc.gpsimd)
        load_stacked("w4s", 8, w4_scales, nc.gpsimd)
        load_list("list2", offs2)
        load_table("t2w0", tab2_words[0])
        load_beside("t2s", 0, tab2_scales)
        load_weight("w1_00", w1_0, 0)
        load_w2()
        load_beside("w2s", 0, w2_scales)
        load_table("t2w1", tab2_words[1])
        load_list("list1", offs)
        gather("v2w0", U32, sb["t2w0"][:].bitcast(U32), "list2")
        gather("v2s0", U8, sb["t2s"][:, 0:1024], "list2")
        gather("v2s1", U8, sb["t2s"][:, 1024:2048], "list2")
        load_weight("w1_10", w1_1, 0)
        load_table("t1w0", tab_words[0])
        load_list("list3", offs3)
        load_beside("t3s", 0, tab3_scales)
        load_table("t1w1", tab_words[1])
        load_weight("w1_01", w1_0, 1)
        load_weight("w1_11", w1_1, 1)
        load_t3w()
        load_weight("w3_0", w3, 0, 0, 256)
        load_w4(0)
        load_weight("w3_0b", w3, 0, 256, 512)
        load_weight("w3_1", w3, 1, 0, 256)
        load_weight("w3_1b", w3, 1, 256, 512)
        load_w4(1)

        cast_weight("w1_00", sc)
        deal("w2d", "w2r", 8)
        deal("w2sd", "w2s", 16)
        gather("v2w1", U32, sb["t2w1"][:].bitcast(U32), "list2", "w2r")
        cast_weight("w1_10", sc)
        quantize("w1_00", over="w2s")
        for g in range(2):
            for t in range(4):
                b_unit(g, t, "raw_w1_10")
        gather("v1s", U8, sb["t1s"][:], "list1")
        gather("v1w0", U32, sb["t1w0"][:].bitcast(U32), "list1")
        gather("v3s", U8, sb["t3s"][:], "list3")
        quantize("w1_10", over="t1s")
        for c in range(4):
            a_pass(0, c, 0)
        gather("v1w1", U32, sb["t1w1"][:].bitcast(U32), "list1", None, 0, 256)
        gather("v1w1", U32, sb["t1w1"][:].bitcast(U32), "list1", None, 256, 512)
        cast_weight("w1_01", sc)
        for c in range(4):
            a_pass(0, c, 1)
            product(0, c)
        cast_weight("w1_11", sc)
        quantize("w1_01")
        for c in range(4):
            a_pass(1, c, 0)
        gather("v3w", U16, sb["t3w"][:], "list3")
        quantize("w1_11")
        deal("w4sd", "w4s", 16, "bf_z0")
        quantize("z0", over="raw_w1_01")
        cast_weight("w3_0", sc, 0, 64)
        cast_weight("w3_0", sc, 64, 128, "w3_0b", 64)
        for c in range(4):
            a_pass(1, c, 1)
        cast_weight("w3_1", sc, 0, 64)
        deal("w4d0", "w4r0", 4)
        for u in range(2):
            q_pass(0, 0, u, 0)
        product(1, 0, "w4r0")
        product(1, 1)
        quantize("w3_0")
        quantize("z1", 0, 256)
        lim_unit(0, 0, 0, "raw_w3_1")
        lim_unit(0, 0, 1)
        cast_weight("w3_1", sc, 64, 128, "w3_1b", 64)
        lim_unit(0, 1, 0, "raw_w3_1b")
        lim_unit(0, 1, 1)
        deal("w4d1", "w4r1", 4, "c_w3_0", sc, U32)
        product(1, 2)
        product(1, 3)
        quantize("z1", 256, 512)

        for u in range(2):
            q_pass(0, 0, u, 1)
            q_min(0, 0, u, "bf_w1_11")
        quantize("w3_1")
        q_max(0, 0)
        for hh in range(2):
            for u in range(2):
                lim_unit(1, hh, u, "w4r1" if hh == 0 else None)
        round_y(0, 0, sc)
        for u in range(2):
            q_pass(0, 1, u, 0)
            q_pass(0, 1, u, 1)
            q_min(0, 1, u, "t1w1")
        q_max(0, 1)
        round_y(0, 1, sc)
        for u in range(2):
            q_pass(1, 0, u, 0)
            q_pass(1, 0, u, 1)
            q_min(1, 0, u, "raw_w1_00")
        planes(0, 0, 256)
        q_max(1, 0)
        round_y(1, 0, sc)
        for u in range(2):
            q_pass(1, 1, u, 0)
            q_pass(1, 1, u, 1)
            q_min(1, 1, u, "raw_w3_0")
        planes(0, 256, S)
        q_max(1, 1, slice(0, 2))
        q_max(1, 1, slice(2, 4))
        planes(1, 0, 256)
        round_y(1, 1, vc)
        planes(1, 256, S)
        store_scales()
